import numpy as np
import ml_dtypes


def mxq(x, axis, fmt="e4m3"):
    dtype, down = {"e4m3": (ml_dtypes.float8_e4m3fn, 7), "e5m2": (ml_dtypes.float8_e5m2, 14)}[fmt]
    v = np.moveaxis(np.asarray(x, np.float32).astype(ml_dtypes.bfloat16).astype(np.float64), axis, -1)
    blocks = v.reshape(v.shape[:-1] + (-1, 32))
    amax = np.abs(blocks).max(-1, keepdims=True)
    byte = np.maximum(np.where(amax > 0, np.frexp(amax)[1] - 1 + 127, 0) - down, 1)
    scale = np.exp2(byte - 127.0)
    codes = (blocks / scale).astype(np.float32).astype(dtype).astype(np.float64)
    return np.moveaxis((codes * scale).reshape(v.shape), -1, axis)


WIDE = False


def mx_kscale(k):
    if not WIDE:
        return np.ones(k)
    levels = np.array([10, -10, 5, -5, 0])
    if k % 512:
        return np.exp2(np.random.permutation(np.resize(levels, k // 32))).repeat(32)
    a = np.empty((k // 512, 16))
    for p in range(k // 512):
        a[p, :8] = np.random.permutation(np.resize(levels, 8))
        for g in range(8):
            far = levels[np.abs(levels - a[p, g]) >= 10]
            a[p, g + 8] = far[np.random.randint(len(far))]
    return np.exp2(a.ravel()).repeat(32)


def f64(x):
    return np.asarray(x).astype(np.float64)


def striped(idx):
    return np.tile(idx.reshape(-1, 16).T, (8, 1)).astype(np.uint16)


def unstriped(offs):
    return offs[:16].T.reshape(-1).astype(np.int64)


def pack_weight(w):
    k, n = w.shape
    w = f64(np.asarray(w, np.float32).astype(ml_dtypes.bfloat16)).reshape(k // 32, 32, n)
    amax = np.abs(w).max(1)
    byte = np.clip(np.where(amax > 0, np.frexp(amax)[1] - 1 + 127 - 7, 1), 1, 254)
    scaled = (w * np.exp2(127.0 - byte)[:, None, :]).reshape(k, n).astype(np.float32)
    words = np.ascontiguousarray(scaled.reshape(k // 512, 128, 4, n).transpose(0, 1, 3, 2)).astype(ml_dtypes.float8_e4m3fn).view(np.uint8)
    return words, np.ascontiguousarray(byte.astype(np.uint8).reshape(k // 512, 16, n))


def unpack_weight(words, scales):
    g, p, n, _ = words.shape
    vals = np.ascontiguousarray(words).view(ml_dtypes.float8_e4m3fn).astype(np.float64) * np.repeat(np.exp2(scales.astype(np.float64) - 127.0), 8, axis=1)[..., None]
    return vals.transpose(0, 1, 3, 2).reshape(g * 512, n)


def planes(y):
    n, m = y.shape
    v = y.astype(np.float32).astype(ml_dtypes.bfloat16).astype(np.float64).reshape(n // 32, 32, m)
    top = np.abs(v).max(1)
    byte = np.clip(np.where(top > 0, np.frexp(top)[1] - 1 + 127 - 7, 1), 1, 254)
    codes = (v * np.exp2(127.0 - byte)[:, None, :]).reshape(n, m).astype(np.float32).astype(ml_dtypes.float8_e4m3fn).view(np.uint8)
    words = codes.reshape(n // 512, 128, 4, m).transpose(0, 1, 3, 2)
    return np.ascontiguousarray(words), np.ascontiguousarray(byte.astype(np.uint8).reshape(n // 512, 16, m))


def silu(v):
    return v / (1.0 + np.exp(-np.maximum(v, -700.0)))


K, T, S, H, N = 512, 1024, 512, 512, 512


def setup_inputs():
    n = np.random.standard_normal
    s = mx_kscale(K)[:, None]
    u = mx_kscale(H)
    packed_xT = pack_weight(n((K, T)) * s)
    return {
        "x_words": packed_xT[0],
        "x_scales": packed_xT[1],
        "eT": (n((K, S)) * s).astype(np.float32),
        "w1": (n((K, H)) / np.sqrt(3 * K) / s * u).astype(np.float32),
        "w2": (n((K, H)) / np.sqrt(3 * K) / s * u).astype(np.float32),
        "w3": (n((K, H)) / np.sqrt(3 * K) / s * u).astype(np.float32),
        "w4": (n((H, N)) / np.sqrt(H) / u[:, None]).astype(np.float32),
        "offs": striped(np.random.permutation(T)[:S]),
        "dst": striped(np.random.permutation(T)[:S]),
    }


def reference(x_words, x_scales, eT, w1, w2, w3, w4, offs, dst):
    xq = unpack_weight(x_words, x_scales)[:, unstriped(offs)]
    x_dst = unpack_weight(x_words, x_scales)[:, unstriped(dst)]
    eTq = mxq(f64(eT), 0, "e4m3")
    h = silu(mxq(f64(w1), 0, "e4m3").T @ xq + mxq(f64(w2), 0, "e4m3").T @ x_dst + mxq(f64(w3), 0, "e4m3").T @ eTq)
    out_0 = mxq(f64(w4), 0, "e4m3").T @ mxq(h, 0, "e4m3")
    return (out_0,) + planes(out_0)

@@ -1,0 +1,171 @@
+from contextlib import ExitStack
+
+import concourse.mybir as mybir
+
+K, T, S, H, N = 512, 1024, 512, 512, 512
+FLOPS = 2 * K * H * S * 3 + 2 * H * N * S
+
+F32 = mybir.dt.float32
+BF16 = mybir.dt.bfloat16
+I32 = mybir.dt.int32
+U32 = mybir.dt.uint32
+U16 = mybir.dt.uint16
+U8 = mybir.dt.uint8
+FP8X4 = mybir.dt.float8_e4m3fn_x4
+SILU = mybir.ActivationFunctionType.Silu
+
+P = 128
+PACK = 4
+CHUNK = 128
+CHUNKS = S // CHUNK
+
+
+def tile_picked_zedge_silu_po_kernel(tc, x_words, x_scales, eT, w1, w2, w3, w4, offs, dst, out_0, out_1, out_2):
+    nc = tc.nc
+    with ExitStack() as ctx:
+        lists = ctx.enter_context(tc.tile_pool(name="lists", bufs=1))
+        keep = ctx.enter_context(tc.tile_pool(name="keep", bufs=1))
+        psum = ctx.enter_context(tc.psum_pool(name="psum", bufs=1))
+
+        def sb(shape, dtype, name):
+            return keep.tile(shape, dtype, name=name, align_bytes=64)
+
+        warm_in = sb([P, 1], F32, "warm_in")
+        warm_out = sb([P, 1], F32, "warm_out")
+        nc.vector.memset(warm_in[:], 0.0)
+        nc.scalar.activation(warm_out[:], warm_in[:], SILU)
+
+        node_scales = sb([P, T], U8, "node_scales")
+        nc.vector.memset(node_scales[:].bitcast(I32), 0)
+
+        node_words = sb([P, T], U32, "node_words")
+        nc.sync.dma_start(node_words[:].bitcast(I32), x_words[0].rearrange("p n t -> p (n t)").bitcast(I32))
+        senders = lists.tile([P, S // 16], U16, name="senders")
+        receivers = lists.tile([P, S // 16], U16, name="receivers")
+        nc.sync.dma_start(senders[:], offs)
+        nc.sync.dma_start(receivers[:], dst)
+        for q in range(4):
+            nc.sync.dma_start(node_scales[32 * q : 32 * q + 4, :].bitcast(I32), x_scales[0, 4 * q : 4 * q + 4, :].bitcast(I32))
+
+        def load_weight(w, name):
+            raw = sb([P, PACK, H], F32, name)
+            nc.sync.dma_start(raw[:], w.rearrange("(p j) c -> p j c", j=PACK))
+            return raw
+
+        w1_raw = load_weight(w1, "w1_raw")
+        w2_raw = load_weight(w2, "w2_raw")
+        w3_raw = load_weight(w3, "w3_raw")
+        e_rows = eT.rearrange("(p j) n -> p j n", j=PACK)
+        e_raw = []
+        for half in range(2):
+            raw = sb([P, PACK, S // 2], F32, f"e_raw{half}")
+            nc.sync.dma_start(raw[:], e_rows[:, :, half * (S // 2) : (half + 1) * (S // 2)])
+            e_raw.append(raw)
+        w4_raw = load_weight(w4, "w4_raw")
+
+        picked = []
+        for name, offsets in (("sender", senders), ("receiver", receivers)):
+            words = sb([P, S], U32, name + "_words")
+            nc.vector.tensor_copy(words[:], node_words[:].indirect(offsets[:]))
+            picked.append([words])
+        for i, (name, offsets) in enumerate((("sender", senders), ("receiver", receivers))):
+            scales = sb([P, S], U8, name + "_scales")
+            nc.vector.tensor_copy(scales[:], node_scales[:].indirect(offsets[:]))
+            picked[i].append(scales)
+
+        def quantize_weight(raw, name, on_scalar, calls):
+            dealt = sb([P, PACK * H], BF16, name + "_dealt")
+            dst_view = dealt[:].rearrange("p (t m j) -> p m j t", t=PACK, j=PACK)
+            src_view = raw[:].rearrange("p j (m t) -> p m j t", t=PACK)
+            if on_scalar > 0:
+                nc.scalar.copy(dst_view[:, :on_scalar], src_view[:, :on_scalar])
+            if on_scalar < P:
+                nc.vector.tensor_copy(dst_view[:, on_scalar:], src_view[:, on_scalar:])
+            words = sb([P, H], U32, name + "_words")
+            scales = sb([P, H], U8, name + "_scales")
+            width = H // calls
+            for c in range(calls):
+                cols = slice(c * width, (c + 1) * width)
+                nc.vector.quantize_mx(
+                    out=words[:, cols].bitcast(FP8X4),
+                    scales=scales[:, cols],
+                    in_=dealt[:, PACK * c * width : PACK * (c + 1) * width],
+                )
+            return words, scales
+
+        w1_q = quantize_weight(w1_raw, "w1", 128, 1)
+        w2_q = quantize_weight(w2_raw, "w2", 64, 1)
+        w3_q = quantize_weight(w3_raw, "w3", 40, 2)
+
+        def weave(dst_tile, src, copy=nc.vector.tensor_copy):
+            copy(
+                dst_tile[:].rearrange("p (c i t) -> p c t i", i=4, t=PACK),
+                src.rearrange("p t (c i) -> p c t i", i=4),
+            )
+
+        e_words = sb([P, S], U32, "e_words")
+        e_scales = sb([P, S], U8, "e_scales")
+        h_words = sb([P, S], U32, "h_words")
+        h_scales = sb([P, S], U8, "h_scales")
+        for c in range(CHUNKS):
+            cols = slice(c * CHUNK, (c + 1) * CHUNK)
+            woven = sb([P, PACK * CHUNK], BF16, f"e_woven{c}")
+            weave(woven, e_raw[c // 2][:, :, (c % 2) * CHUNK : (c % 2 + 1) * CHUNK], nc.vector.tensor_copy if c == 0 else nc.scalar.copy)
+            nc.vector.quantize_mx(out=e_words[:, cols].bitcast(FP8X4), scales=e_scales[:, cols], in_=woven[:])
+
+        w4_q = quantize_weight(w4_raw, "w4", 32, 2)
+        moving = [picked[1], picked[0], [e_words, e_scales]]
+        stationary = [w2_q, w1_q, w3_q]
+        for c in range(CHUNKS):
+            cols = slice(c * CHUNK, (c + 1) * CHUNK)
+            pre = psum.tile([P, PACK, CHUNK], F32, name=f"pre{c}")
+            for t in range(PACK):
+                rows = slice(t * P, (t + 1) * P)
+                for g in range(3):
+                    nc.tensor.matmul_mx(
+                        out=pre[:, t, :],
+                        lhsT=stationary[g][0][:, rows].bitcast(FP8X4),
+                        lhsT_scale=stationary[g][1][:, rows],
+                        rhs=moving[g][0][:, cols].bitcast(FP8X4),
+                        rhs_scale=moving[g][1][:, cols],
+                        start=(g == 0),
+                        stop=(g == 2),
+                    )
+            hidden = sb([P, PACK * CHUNK], BF16, f"hidden{c}")
+            nc.scalar.activation(
+                hidden[:].rearrange("p (n t) -> p n t", t=PACK), pre[:].rearrange("p t n -> p n t"), SILU
+            )
+            nc.vector.quantize_mx(out=h_words[:, cols].bitcast(FP8X4), scales=h_scales[:, cols], in_=hidden[:])
+
+
+        y_words = sb([P, S], U32, "y_words")
+        y_scales = sb([P, S], U8, "y_scales")
+        out_rows = out_0.rearrange("(p t) n -> p t n", t=PACK)
+        out_words = out_1[0].rearrange("p n t -> p (n t)").bitcast(I32)
+        for c in range(CHUNKS):
+            cols = slice(c * CHUNK, (c + 1) * CHUNK)
+            acc = psum.tile([P, PACK, CHUNK], F32, name=f"acc{c}")
+            for t in range(PACK):
+                rows = slice(t * P, (t + 1) * P)
+                nc.tensor.matmul_mx(
+                    out=acc[:, t, :],
+                    lhsT=w4_q[0][:, rows].bitcast(FP8X4),
+                    lhsT_scale=w4_q[1][:, rows],
+                    rhs=h_words[:, cols].bitcast(FP8X4),
+                    rhs_scale=h_scales[:, cols],
+                    start=True,
+                    stop=True,
+                )
+            y = sb([P, PACK, CHUNK], F32, f"y{c}")
+            nc.scalar.copy(y[:], acc[:])
+            nc.sync.dma_start(out_rows[:, :, cols], y[:])
+            woven = sb([P, PACK * CHUNK], BF16, f"y_woven{c}")
+            weave(woven, y[:])
+            nc.vector.quantize_mx(out=y_words[:, cols].bitcast(FP8X4), scales=y_scales[:, cols], in_=woven[:])
+            if c == CHUNKS - 2:
+                nc.sync.dma_start(out_words[:, : (c + 1) * CHUNK], y_words[:, : (c + 1) * CHUNK].bitcast(I32))
+        last = slice(S - CHUNK, S)
+        nc.sync.dma_start(out_words[:, last], y_words[:, last].bitcast(I32))
+        for q in range(4):
+            queue = nc.sync if q % 2 == 0 else nc.scalar
+            queue.dma_start(out_2[0, 4 * q : 4 * q + 4, :].bitcast(I32), y_scales[32 * q : 32 * q + 4, :].bitcast(I32))

@@ -27,8 +27,8 @@ def tile_picked_zedge_silu_po_kernel(tc, x_words, x_scales, eT, w1, w2, w3, w4, 
         keep = ctx.enter_context(tc.tile_pool(name="keep", bufs=1))
         psum = ctx.enter_context(tc.psum_pool(name="psum", bufs=1))
 
-        def sb(shape, dtype, name):
-            return keep.tile(shape, dtype, name=name, align_bytes=64)
+        def sb(shape, dtype, name, tag=None):
+            return keep.tile(shape, dtype, name=name, tag=tag or name, align_bytes=64)
 
         warm_in = sb([P, 1], F32, "warm_in")
         warm_out = sb([P, 1], F32, "warm_out")
@@ -54,14 +54,18 @@ def tile_picked_zedge_silu_po_kernel(tc, x_words, x_scales, eT, w1, w2, w3, w4, 
 
         w1_raw = load_weight(w1, "w1_raw")
         w2_raw = load_weight(w2, "w2_raw")
-        w3_raw = load_weight(w3, "w3_raw")
         e_rows = eT.rearrange("(p j) n -> p j n", j=PACK)
-        e_raw = []
+        e_first = sb([P, PACK, CHUNK], F32, "e_first")
+        nc.sync.dma_start(e_first[:], e_rows[:, :, :CHUNK])
+        w3_raw = load_weight(w3, "w3_raw")
+        e_rest = sb([P, PACK, S - CHUNK], F32, "e_rest")
+        nc.sync.dma_start(e_rest[:], e_rows[:, :, CHUNK:])
+        w4_rows = w4.rearrange("(p j) c -> p j c", j=PACK)
+        w4_raw = []
         for half in range(2):
-            raw = sb([P, PACK, S // 2], F32, f"e_raw{half}")
-            nc.sync.dma_start(raw[:], e_rows[:, :, half * (S // 2) : (half + 1) * (S // 2)])
-            e_raw.append(raw)
-        w4_raw = load_weight(w4, "w4_raw")
+            raw = sb([P, PACK, N // 2], F32, f"w4_raw{half}")
+            nc.sync.dma_start(raw[:], w4_rows[:, :, half * (N // 2) : (half + 1) * (N // 2)])
+            w4_raw.append(raw)
 
         picked = []
         for name, offsets in (("sender", senders), ("receiver", receivers)):
@@ -73,14 +77,15 @@ def tile_picked_zedge_silu_po_kernel(tc, x_words, x_scales, eT, w1, w2, w3, w4, 
             nc.vector.tensor_copy(scales[:], node_scales[:].indirect(offsets[:]))
             picked[i].append(scales)
 
-        def quantize_weight(raw, name, on_scalar, calls):
+        def quantize_weight(parts, name, calls):
             dealt = sb([P, PACK * H], BF16, name + "_dealt")
             dst_view = dealt[:].rearrange("p (t m j) -> p m j t", t=PACK, j=PACK)
-            src_view = raw[:].rearrange("p j (m t) -> p m j t", t=PACK)
-            if on_scalar > 0:
-                nc.scalar.copy(dst_view[:, :on_scalar], src_view[:, :on_scalar])
-            if on_scalar < P:
-                nc.vector.tensor_copy(dst_view[:, on_scalar:], src_view[:, on_scalar:])
+            first = 0
+            for copy, src in parts:
+                src_view = src.rearrange("p j (m t) -> p m j t", t=PACK)
+                count = src.shape[2] // PACK
+                copy(dst_view[:, first : first + count], src_view)
+                first = first + count
             words = sb([P, H], U32, name + "_words")
             scales = sb([P, H], U8, name + "_scales")
             width = H // calls
@@ -93,9 +98,8 @@ def tile_picked_zedge_silu_po_kernel(tc, x_words, x_scales, eT, w1, w2, w3, w4, 
                 )
             return words, scales
 
-        w1_q = quantize_weight(w1_raw, "w1", 128, 1)
-        w2_q = quantize_weight(w2_raw, "w2", 64, 1)
-        w3_q = quantize_weight(w3_raw, "w3", 40, 2)
+        w1_q = quantize_weight([(nc.scalar.copy, w1_raw[:])], "w1", 1)
+        w2_q = quantize_weight([(nc.scalar.copy, w2_raw[:, :, :256]), (nc.vector.tensor_copy, w2_raw[:, :, 256:])], "w2", 1)
 
         def weave(dst_tile, src, copy=nc.vector.tensor_copy):
             copy(
@@ -105,15 +109,23 @@ def tile_picked_zedge_silu_po_kernel(tc, x_words, x_scales, eT, w1, w2, w3, w4, 
 
         e_words = sb([P, S], U32, "e_words")
         e_scales = sb([P, S], U8, "e_scales")
-        h_words = sb([P, S], U32, "h_words")
         h_scales = sb([P, S], U8, "h_scales")
-        for c in range(CHUNKS):
+
+        def quantize_edges(c, src, copy):
             cols = slice(c * CHUNK, (c + 1) * CHUNK)
             woven = sb([P, PACK * CHUNK], BF16, f"e_woven{c}")
-            weave(woven, e_raw[c // 2][:, :, (c % 2) * CHUNK : (c % 2 + 1) * CHUNK], nc.vector.tensor_copy if c == 0 else nc.scalar.copy)
+            weave(woven, src, copy)
             nc.vector.quantize_mx(out=e_words[:, cols].bitcast(FP8X4), scales=e_scales[:, cols], in_=woven[:])
 
-        w4_q = quantize_weight(w4_raw, "w4", 32, 2)
+        quantize_edges(0, e_first[:], nc.vector.tensor_copy)
+        w3_q = quantize_weight([(nc.scalar.copy, w3_raw[:, :, :160]), (nc.vector.tensor_copy, w3_raw[:, :, 160:])], "w3", 4)
+        for c in range(1, CHUNKS):
+            quantize_edges(c, e_rest[:, :, (c - 1) * CHUNK : c * CHUNK], nc.scalar.copy if c == 1 else nc.vector.tensor_copy)
+
+        w4_q = quantize_weight([(nc.vector.tensor_copy, raw[:]) for raw in w4_raw], "w4", 2)
+        h_first = sb([P, CHUNK], U32, "h_first")
+        h_rest = sb([P, S - CHUNK], U32, "h_rest", tag="w4_dealt")
+        h_words = [h_first[:]] + [h_rest[:, c * CHUNK : (c + 1) * CHUNK] for c in range(CHUNKS - 1)]
         moving = [picked[1], picked[0], [e_words, e_scales]]
         stationary = [w2_q, w1_q, w3_q]
         for c in range(CHUNKS):
@@ -135,7 +147,7 @@ def tile_picked_zedge_silu_po_kernel(tc, x_words, x_scales, eT, w1, w2, w3, w4, 
             nc.scalar.activation(
                 hidden[:].rearrange("p (n t) -> p n t", t=PACK), pre[:].rearrange("p t n -> p n t"), SILU
             )
-            nc.vector.quantize_mx(out=h_words[:, cols].bitcast(FP8X4), scales=h_scales[:, cols], in_=hidden[:])
+            nc.vector.quantize_mx(out=h_words[c].bitcast(FP8X4), scales=h_scales[:, cols], in_=hidden[:])
 
 
         y_words = sb([P, S], U32, "y_words")
@@ -151,16 +163,19 @@ def tile_picked_zedge_silu_po_kernel(tc, x_words, x_scales, eT, w1, w2, w3, w4, 
                     out=acc[:, t, :],
                     lhsT=w4_q[0][:, rows].bitcast(FP8X4),
                     lhsT_scale=w4_q[1][:, rows],
-                    rhs=h_words[:, cols].bitcast(FP8X4),
+                    rhs=h_words[c].bitcast(FP8X4),
                     rhs_scale=h_scales[:, cols],
                     start=True,
                     stop=True,
                 )
             y = sb([P, PACK, CHUNK], F32, f"y{c}")
-            nc.scalar.copy(y[:], acc[:])
-            nc.sync.dma_start(out_rows[:, :, cols], y[:])
             woven = sb([P, PACK * CHUNK], BF16, f"y_woven{c}")
-            weave(woven, y[:])
+            if c == CHUNKS - 1:
+                nc.scalar.copy(woven[:].rearrange("p (n t) -> p n t", t=PACK), acc[:].rearrange("p t n -> p n t"))
+            (nc.vector.tensor_copy if c == 1 else nc.scalar.copy)(y[:], acc[:])
+            nc.sync.dma_start(out_rows[:, :, cols], y[:])
+            if c < CHUNKS - 1:
+                weave(woven, y[:])
             nc.vector.quantize_mx(out=y_words[:, cols].bitcast(FP8X4), scales=y_scales[:, cols], in_=woven[:])
             if c == CHUNKS - 2:
                 nc.sync.dma_start(out_words[:, : (c + 1) * CHUNK], y_words[:, : (c + 1) * CHUNK].bitcast(I32))

@@ -79,10 +79,10 @@ def tile_picked_zedge_silu_po_kernel(tc, x_words, x_scales, eT, w1, w2, w3, w4, 
 
         def quantize_weight(parts, name, calls):
             dealt = sb([P, PACK * H], BF16, name + "_dealt")
-            dst_view = dealt[:].rearrange("p (t m j) -> p m j t", t=PACK, j=PACK)
+            dst_view = dealt[:].rearrange("p (t m j) -> p m t j", t=PACK, j=PACK)
             first = 0
             for copy, src in parts:
-                src_view = src.rearrange("p j (m t) -> p m j t", t=PACK)
+                src_view = src.rearrange("p j (m t) -> p m t j", t=PACK)
                 count = src.shape[2] // PACK
                 copy(dst_view[:, first : first + count], src_view)
                 first = first + count
@@ -99,7 +99,7 @@ def tile_picked_zedge_silu_po_kernel(tc, x_words, x_scales, eT, w1, w2, w3, w4, 
             return words, scales
 
         w1_q = quantize_weight([(nc.scalar.copy, w1_raw[:])], "w1", 1)
-        w2_q = quantize_weight([(nc.scalar.copy, w2_raw[:, :, :256]), (nc.vector.tensor_copy, w2_raw[:, :, 256:])], "w2", 1)
+        w2_q = quantize_weight([(nc.scalar.copy, w2_raw[:, :, :288]), (nc.vector.tensor_copy, w2_raw[:, :, 288:])], "w2", 1)
 
         def weave(dst_tile, src, copy=nc.vector.tensor_copy):
             copy(
@@ -117,7 +117,7 @@ def tile_picked_zedge_silu_po_kernel(tc, x_words, x_scales, eT, w1, w2, w3, w4, 
             weave(woven, src, copy)
             nc.vector.quantize_mx(out=e_words[:, cols].bitcast(FP8X4), scales=e_scales[:, cols], in_=woven[:])
 
-        quantize_edges(0, e_first[:], nc.vector.tensor_copy)
+        quantize_edges(0, e_first[:], nc.scalar.copy)
         w3_q = quantize_weight([(nc.scalar.copy, w3_raw[:, :, :160]), (nc.vector.tensor_copy, w3_raw[:, :, 160:])], "w3", 4)
         for c in range(1, CHUNKS):
             quantize_edges(c, e_rest[:, :, (c - 1) * CHUNK : c * CHUNK], nc.scalar.copy if c == 1 else nc.vector.tensor_copy)

@@ -18,6 +18,7 @@ P = 128
 PACK = 4
 CHUNK = 128
 CHUNKS = S // CHUNK
+ALL, LOW, HIGH = slice(0, 4), slice(0, 2), slice(2, 4)
 
 
 def tile_picked_zedge_silu_po_kernel(tc, x_words, x_scales, eT, w1, w2, w3, w4, offs, dst, out_0, out_1, out_2):
@@ -30,13 +31,13 @@ def tile_picked_zedge_silu_po_kernel(tc, x_words, x_scales, eT, w1, w2, w3, w4, 
         def sb(shape, dtype, name, tag=None):
             return keep.tile(shape, dtype, name=name, tag=tag or name, align_bytes=64)
 
+        node_scales = sb([P, T], U8, "node_scales")
+        nc.vector.memset(node_scales[:].bitcast(I32), 0)
+
         warm_in = sb([P, 1], F32, "warm_in")
         warm_out = sb([P, 1], F32, "warm_out")
         nc.vector.memset(warm_in[:], 0.0)
         nc.scalar.activation(warm_out[:], warm_in[:], SILU)
-
-        node_scales = sb([P, T], U8, "node_scales")
-        nc.vector.memset(node_scales[:].bitcast(I32), 0)
 
         node_words = sb([P, T], U32, "node_words")
         nc.sync.dma_start(node_words[:].bitcast(I32), x_words[0].rearrange("p n t -> p (n t)").bitcast(I32))
@@ -47,25 +48,18 @@ def tile_picked_zedge_silu_po_kernel(tc, x_words, x_scales, eT, w1, w2, w3, w4, 
         for q in range(4):
             nc.sync.dma_start(node_scales[32 * q : 32 * q + 4, :].bitcast(I32), x_scales[0, 4 * q : 4 * q + 4, :].bitcast(I32))
 
-        def load_weight(w, name):
-            raw = sb([P, PACK, H], F32, name)
-            nc.sync.dma_start(raw[:], w.rearrange("(p j) c -> p j c", j=PACK))
+        def load(w, name, first, width):
+            raw = sb([P, PACK, width], F32, f"{name}_raw{first}")
+            nc.sync.dma_start(raw[:], w.rearrange("(p j) c -> p j c", j=PACK)[:, :, first : first + width])
             return raw
 
-        w1_raw = load_weight(w1, "w1_raw")
-        w2_raw = load_weight(w2, "w2_raw")
-        e_rows = eT.rearrange("(p j) n -> p j n", j=PACK)
-        e_first = sb([P, PACK, CHUNK], F32, "e_first")
-        nc.sync.dma_start(e_first[:], e_rows[:, :, :CHUNK])
-        w3_raw = load_weight(w3, "w3_raw")
-        e_rest = sb([P, PACK, S - CHUNK], F32, "e_rest")
-        nc.sync.dma_start(e_rest[:], e_rows[:, :, CHUNK:])
-        w4_rows = w4.rearrange("(p j) c -> p j c", j=PACK)
-        w4_raw = []
-        for half in range(2):
-            raw = sb([P, PACK, N // 2], F32, f"w4_raw{half}")
-            nc.sync.dma_start(raw[:], w4_rows[:, :, half * (N // 2) : (half + 1) * (N // 2)])
-            w4_raw.append(raw)
+        w1_raw = load(w1, "w1", 0, H)
+        w2_raw = load(w2, "w2", 0, H)
+        e_first = load(eT, "e", 0, CHUNK)
+        w3_raw = load(w3, "w3", 0, H)
+        e_middle = load(eT, "e", CHUNK, 2 * CHUNK)
+        e_last = load(eT, "e", 3 * CHUNK, CHUNK)
+        w4_raw = [load(w4, "w4", 0, 256), load(w4, "w4", 256, 128), load(w4, "w4", 384, 128)]
 
         picked = []
         for name, offsets in (("sender", senders), ("receiver", receivers)):
@@ -77,15 +71,18 @@ def tile_picked_zedge_silu_po_kernel(tc, x_words, x_scales, eT, w1, w2, w3, w4, 
             nc.vector.tensor_copy(scales[:], node_scales[:].indirect(offsets[:]))
             picked[i].append(scales)
 
-        def quantize_weight(parts, name, calls):
-            dealt = sb([P, PACK * H], BF16, name + "_dealt")
-            dst_view = dealt[:].rearrange("p (t m j) -> p m t j", t=PACK, j=PACK)
-            first = 0
-            for copy, src in parts:
-                src_view = src.rearrange("p j (m t) -> p m t j", t=PACK)
+        def deal(dealt, parts):
+            for copy, src, first, slots in parts:
                 count = src.shape[2] // PACK
-                copy(dst_view[:, first : first + count], src_view)
-                first = first + count
+                copy(
+                    dealt[:].rearrange("p t m j -> p m t j")[:, first : first + count, slots],
+                    src.rearrange("p j (m t) -> p m t j", t=PACK)[:, :, slots],
+                )
+
+        def quantize_weight(parts, name, calls):
+            dealt = sb([P, PACK, P, PACK], BF16, name + "_dealt")
+            deal(dealt, parts)
+            flat = dealt[:].rearrange("p t m j -> p (t m j)")
             words = sb([P, H], U32, name + "_words")
             scales = sb([P, H], U8, name + "_scales")
             width = H // calls
@@ -94,12 +91,12 @@ def tile_picked_zedge_silu_po_kernel(tc, x_words, x_scales, eT, w1, w2, w3, w4, 
                 nc.vector.quantize_mx(
                     out=words[:, cols].bitcast(FP8X4),
                     scales=scales[:, cols],
-                    in_=dealt[:, PACK * c * width : PACK * (c + 1) * width],
+                    in_=flat[:, PACK * c * width : PACK * (c + 1) * width],
                 )
             return words, scales
 
-        w1_q = quantize_weight([(nc.scalar.copy, w1_raw[:])], "w1", 1)
-        w2_q = quantize_weight([(nc.scalar.copy, w2_raw[:, :, :288]), (nc.vector.tensor_copy, w2_raw[:, :, 288:])], "w2", 1)
+        w1_q = quantize_weight([(nc.scalar.copy, w1_raw[:], 0, ALL)], "w1", 1)
+        w2_q = quantize_weight([(nc.scalar.copy, w2_raw[:], 0, LOW), (nc.vector.tensor_copy, w2_raw[:], 0, HIGH)], "w2", 1)
 
         def weave(dst_tile, src, copy=nc.vector.tensor_copy):
             copy(
@@ -118,51 +115,77 @@ def tile_picked_zedge_silu_po_kernel(tc, x_words, x_scales, eT, w1, w2, w3, w4, 
             nc.vector.quantize_mx(out=e_words[:, cols].bitcast(FP8X4), scales=e_scales[:, cols], in_=woven[:])
 
         quantize_edges(0, e_first[:], nc.scalar.copy)
-        w3_q = quantize_weight([(nc.scalar.copy, w3_raw[:, :, :160]), (nc.vector.tensor_copy, w3_raw[:, :, 160:])], "w3", 4)
-        for c in range(1, CHUNKS):
-            quantize_edges(c, e_rest[:, :, (c - 1) * CHUNK : c * CHUNK], nc.scalar.copy if c == 1 else nc.vector.tensor_copy)
+        w3_q = quantize_weight(
+            [
+                (nc.vector.tensor_copy, w3_raw[:], 0, LOW),
+                (nc.scalar.copy, w3_raw[:], 0, HIGH),
+            ],
+            "w3",
+            4,
+        )
+        quantize_edges(1, e_middle[:, :, :CHUNK], nc.scalar.copy)
+        quantize_edges(2, e_middle[:, :, CHUNK:], nc.scalar.copy)
+        quantize_edges(3, e_last[:], nc.vector.tensor_copy)
 
-        w4_q = quantize_weight([(nc.vector.tensor_copy, raw[:]) for raw in w4_raw], "w4", 2)
-        h_first = sb([P, CHUNK], U32, "h_first")
-        h_rest = sb([P, S - CHUNK], U32, "h_rest", tag="w4_dealt")
-        h_words = [h_first[:]] + [h_rest[:, c * CHUNK : (c + 1) * CHUNK] for c in range(CHUNKS - 1)]
-        moving = [picked[1], picked[0], [e_words, e_scales]]
-        stationary = [w2_q, w1_q, w3_q]
-        for c in range(CHUNKS):
-            cols = slice(c * CHUNK, (c + 1) * CHUNK)
-            pre = psum.tile([P, PACK, CHUNK], F32, name=f"pre{c}")
+        w4_words = sb([P, N], U32, "w4_words")
+        w4_scales = sb([P, N], U8, "w4_scales")
+
+        def quantize_w4_half(half, parts):
+            dealt = sb([P, PACK, 64, PACK], BF16, f"w4_dealt{half}")
+            deal(dealt, parts)
             for t in range(PACK):
-                rows = slice(t * P, (t + 1) * P)
+                cols = slice(t * P + half * 64, t * P + (half + 1) * 64)
+                nc.vector.quantize_mx(
+                    out=w4_words[:, cols].bitcast(FP8X4),
+                    scales=w4_scales[:, cols],
+                    in_=dealt[:, t].rearrange("p m j -> p (m j)"),
+                )
+
+        moving = [picked[0], picked[1], [e_words, e_scales]]
+        stationary = [w1_q, w2_q, w3_q]
+        pre = [psum.tile([P, PACK, CHUNK], F32, name=f"pre{c}") for c in range(CHUNKS)]
+
+        accs = [psum.tile([P, PACK, CHUNK], F32, name=f"acc{c}") for c in range(CHUNKS)]
+
+        def first_pass(c, t, g):
+            cols = slice(c * CHUNK, (c + 1) * CHUNK)
+            rows = slice(t * P, (t + 1) * P)
+            nc.tensor.matmul_mx(
+                out=pre[c][:, t, :],
+                lhsT=stationary[g][0][:, rows].bitcast(FP8X4),
+                lhsT_scale=stationary[g][1][:, rows],
+                rhs=moving[g][0][:, cols].bitcast(FP8X4),
+                rhs_scale=moving[g][1][:, cols],
+                start=(g == 0),
+                stop=(g == 2),
+            )
+
+        def first_layer(c):
+            cols = slice(c * CHUNK, (c + 1) * CHUNK)
+            first_pass(c, 0, 2)
+            for t in range(1, PACK):
                 for g in range(3):
-                    nc.tensor.matmul_mx(
-                        out=pre[:, t, :],
-                        lhsT=stationary[g][0][:, rows].bitcast(FP8X4),
-                        lhsT_scale=stationary[g][1][:, rows],
-                        rhs=moving[g][0][:, cols].bitcast(FP8X4),
-                        rhs_scale=moving[g][1][:, cols],
-                        start=(g == 0),
-                        stop=(g == 2),
-                    )
-            hidden = sb([P, PACK * CHUNK], BF16, f"hidden{c}")
+                    first_pass(c, t, g)
+            hidden = sb([P, PACK * CHUNK], BF16, f"hidden{c}", tag="e_raw128" if c == 0 else None)
             nc.scalar.activation(
-                hidden[:].rearrange("p (n t) -> p n t", t=PACK), pre[:].rearrange("p t n -> p n t"), SILU
+                hidden[:].rearrange("p (n t) -> p n t", t=PACK), pre[c][:].rearrange("p t n -> p n t"), SILU
             )
             nc.vector.quantize_mx(out=h_words[c].bitcast(FP8X4), scales=h_scales[:, cols], in_=hidden[:])
-
 
         y_words = sb([P, S], U32, "y_words")
         y_scales = sb([P, S], U8, "y_scales")
         out_rows = out_0.rearrange("(p t) n -> p t n", t=PACK)
         out_words = out_1[0].rearrange("p n t -> p (n t)").bitcast(I32)
-        for c in range(CHUNKS):
+
+        def second_layer(c, copy):
             cols = slice(c * CHUNK, (c + 1) * CHUNK)
-            acc = psum.tile([P, PACK, CHUNK], F32, name=f"acc{c}")
+            acc = accs[c]
             for t in range(PACK):
                 rows = slice(t * P, (t + 1) * P)
                 nc.tensor.matmul_mx(
                     out=acc[:, t, :],
-                    lhsT=w4_q[0][:, rows].bitcast(FP8X4),
-                    lhsT_scale=w4_q[1][:, rows],
+                    lhsT=w4_words[:, rows].bitcast(FP8X4),
+                    lhsT_scale=w4_scales[:, rows],
                     rhs=h_words[c].bitcast(FP8X4),
                     rhs_scale=h_scales[:, cols],
                     start=True,
@@ -172,11 +195,42 @@ def tile_picked_zedge_silu_po_kernel(tc, x_words, x_scales, eT, w1, w2, w3, w4, 
             woven = sb([P, PACK * CHUNK], BF16, f"y_woven{c}")
             if c == CHUNKS - 1:
                 nc.scalar.copy(woven[:].rearrange("p (n t) -> p n t", t=PACK), acc[:].rearrange("p t n -> p n t"))
-            (nc.vector.tensor_copy if c == 1 else nc.scalar.copy)(y[:], acc[:])
+            copy(y[:], acc[:])
             nc.sync.dma_start(out_rows[:, :, cols], y[:])
+            return y, woven
+
+        def planes(c, y, woven):
+            cols = slice(c * CHUNK, (c + 1) * CHUNK)
             if c < CHUNKS - 1:
                 weave(woven, y[:])
             nc.vector.quantize_mx(out=y_words[:, cols].bitcast(FP8X4), scales=y_scales[:, cols], in_=woven[:])
+
+        for c in range(CHUNKS):
+            first_pass(c, 0, 0)
+        for i in range(6):
+            nc.tensor.matmul_mx(
+                out=accs[i % CHUNKS][:, i // CHUNKS, :],
+                lhsT=w1_q[0][:, :P].bitcast(FP8X4),
+                lhsT_scale=w1_q[1][:, :P],
+                rhs=picked[0][0][:, :CHUNK].bitcast(FP8X4),
+                rhs_scale=picked[0][1][:, :CHUNK],
+                start=True,
+                stop=True,
+            )
+        for c in range(CHUNKS):
+            first_pass(c, 0, 1)
+        quantize_w4_half(0, [(nc.vector.tensor_copy, w4_raw[0][:], 0, ALL)])
+        quantize_w4_half(1, [(nc.vector.tensor_copy, w4_raw[1][:], 0, ALL), (nc.vector.tensor_copy, w4_raw[2][:], 32, ALL)])
+        h_first = sb([P, CHUNK], U32, "h_first", tag="w4_dealt0")
+        h_rest = sb([P, S - CHUNK], U32, "h_rest", tag="w4_dealt1")
+        h_words = [h_first[:]] + [h_rest[:, c * CHUNK : (c + 1) * CHUNK] for c in range(CHUNKS - 1)]
+        for c in range(CHUNKS):
+            first_layer(c)
+        ys = []
+        for c in range(CHUNKS):
+            ys.append(second_layer(c, nc.vector.tensor_copy if c == 1 else nc.scalar.copy))
+        for c in range(CHUNKS):
+            planes(c, *ys[c])
             if c == CHUNKS - 2:
                 nc.sync.dma_start(out_words[:, : (c + 1) * CHUNK], y_words[:, : (c + 1) * CHUNK].bitcast(I32))
         last = slice(S - CHUNK, S)

@@ -18,7 +18,7 @@ P = 128
 PACK = 4
 CHUNK = 128
 CHUNKS = S // CHUNK
-ALL, LOW, HIGH = slice(0, 4), slice(0, 2), slice(2, 4)
+ALL, LOW, HIGH = slice(0, 2), slice(0, 1), slice(1, 2)
 
 
 def tile_picked_zedge_silu_po_kernel(tc, x_words, x_scales, eT, w1, w2, w3, w4, offs, dst, out_0, out_1, out_2):
@@ -75,8 +75,8 @@ def tile_picked_zedge_silu_po_kernel(tc, x_words, x_scales, eT, w1, w2, w3, w4, 
             for copy, src, first, slots in parts:
                 count = src.shape[2] // PACK
                 copy(
-                    dealt[:].rearrange("p t m j -> p m t j")[:, first : first + count, slots],
-                    src.rearrange("p j (m t) -> p m t j", t=PACK)[:, :, slots],
+                    dealt[:].rearrange("p (u v) m j -> p u m j v", v=2)[:, slots, first : first + count],
+                    src.rearrange("p j (m u v) -> p u m j v", u=2, v=2)[:, slots],
                 )
 
         def quantize_weight(parts, name, calls):

@@ -100,8 +100,8 @@ def tile_picked_zedge_silu_po_kernel(tc, x_words, x_scales, eT, w1, w2, w3, w4, 
 
         def weave(dst_tile, src, copy=nc.vector.tensor_copy):
             copy(
-                dst_tile[:].rearrange("p (c i t) -> p c t i", i=4, t=PACK),
-                src.rearrange("p t (c i) -> p c t i", i=4),
+                dst_tile.rearrange("p (c i t) -> p c t i", i=2, t=PACK),
+                src.rearrange("p t (c i) -> p c t i", i=2),
             )
 
         e_words = sb([P, S], U32, "e_words")
@@ -111,7 +111,7 @@ def tile_picked_zedge_silu_po_kernel(tc, x_words, x_scales, eT, w1, w2, w3, w4, 
         def quantize_edges(c, src, copy):
             cols = slice(c * CHUNK, (c + 1) * CHUNK)
             woven = sb([P, PACK * CHUNK], BF16, f"e_woven{c}")
-            weave(woven, src, copy)
+            weave(woven[:], src, copy)
             nc.vector.quantize_mx(out=e_words[:, cols].bitcast(FP8X4), scales=e_scales[:, cols], in_=woven[:])
 
         quantize_edges(0, e_first[:], nc.scalar.copy)
@@ -160,49 +160,51 @@ def tile_picked_zedge_silu_po_kernel(tc, x_words, x_scales, eT, w1, w2, w3, w4, 
                 stop=(g == 2),
             )
 
+        hiddens = []
+
         def first_layer(c):
-            cols = slice(c * CHUNK, (c + 1) * CHUNK)
             first_pass(c, 0, 2)
             for t in range(1, PACK):
                 for g in range(3):
                     first_pass(c, t, g)
             hidden = sb([P, PACK * CHUNK], BF16, f"hidden{c}", tag="e_raw128" if c == 0 else None)
+            hiddens.append(hidden)
             nc.scalar.activation(
                 hidden[:].rearrange("p (n t) -> p n t", t=PACK), pre[c][:].rearrange("p t n -> p n t"), SILU
             )
-            nc.vector.quantize_mx(out=h_words[c].bitcast(FP8X4), scales=h_scales[:, cols], in_=hidden[:])
 
         y_words = sb([P, S], U32, "y_words")
         y_scales = sb([P, S], U8, "y_scales")
         out_rows = out_0.rearrange("(p t) n -> p t n", t=PACK)
         out_words = out_1[0].rearrange("p n t -> p (n t)").bitcast(I32)
 
-        def second_layer(c, copy):
+        def second_layer(c, shares):
             cols = slice(c * CHUNK, (c + 1) * CHUNK)
-            acc = accs[c]
-            for t in range(PACK):
-                rows = slice(t * P, (t + 1) * P)
-                nc.tensor.matmul_mx(
-                    out=acc[:, t, :],
-                    lhsT=w4_words[:, rows].bitcast(FP8X4),
-                    lhsT_scale=w4_scales[:, rows],
-                    rhs=h_words[c].bitcast(FP8X4),
-                    rhs_scale=h_scales[:, cols],
-                    start=True,
-                    stop=True,
-                )
+            nc.vector.quantize_mx(out=h_words[c].bitcast(FP8X4), scales=h_scales[:, cols], in_=hiddens[c][:])
             y = sb([P, PACK, CHUNK], F32, f"y{c}")
+            for acc, slots, copy in shares:
+                for t in range(slots.start, slots.stop):
+                    rows = slice(t * P, (t + 1) * P)
+                    nc.tensor.matmul_mx(
+                        out=acc[:, t, :],
+                        lhsT=w4_words[:, rows].bitcast(FP8X4),
+                        lhsT_scale=w4_scales[:, rows],
+                        rhs=h_words[c].bitcast(FP8X4),
+                        rhs_scale=h_scales[:, cols],
+                        start=True,
+                        stop=True,
+                    )
+                copy(y[:, slots], acc[:, slots])
+                nc.sync.dma_start(out_rows[:, slots, cols], y[:, slots])
+            return y
+
+        def planes(c, y):
+            cols = slice(c * CHUNK, (c + 1) * CHUNK)
             woven = sb([P, PACK * CHUNK], BF16, f"y_woven{c}")
             if c == CHUNKS - 1:
-                nc.scalar.copy(woven[:].rearrange("p (n t) -> p n t", t=PACK), acc[:].rearrange("p t n -> p n t"))
-            copy(y[:], acc[:])
-            nc.sync.dma_start(out_rows[:, :, cols], y[:])
-            return y, woven
-
-        def planes(c, y, woven):
-            cols = slice(c * CHUNK, (c + 1) * CHUNK)
-            if c < CHUNKS - 1:
-                weave(woven, y[:])
+                nc.scalar.copy(woven[:].rearrange("p (n t) -> p n t", t=PACK), accs[c][:].rearrange("p t n -> p n t"))
+            else:
+                weave(woven[:], y[:])
             nc.vector.quantize_mx(out=y_words[:, cols].bitcast(FP8X4), scales=y_scales[:, cols], in_=woven[:])
 
         for c in range(CHUNKS):
@@ -226,14 +228,15 @@ def tile_picked_zedge_silu_po_kernel(tc, x_words, x_scales, eT, w1, w2, w3, w4, 
         h_words = [h_first[:]] + [h_rest[:, c * CHUNK : (c + 1) * CHUNK] for c in range(CHUNKS - 1)]
         for c in range(CHUNKS):
             first_layer(c)
-        ys = []
+        spare = psum.tile([P, PACK, CHUNK], F32, name="spare", tag="pre0")
+        ys = [second_layer(0, [(accs[0], slice(0, 2), nc.vector.tensor_copy), (spare, slice(2, 4), nc.scalar.copy)])]
+        for c in range(1, CHUNKS):
+            ys.append(second_layer(c, [(accs[c], slice(0, 4), nc.vector.tensor_copy if c == 1 else nc.scalar.copy)]))
         for c in range(CHUNKS):
-            ys.append(second_layer(c, nc.vector.tensor_copy if c == 1 else nc.scalar.copy))
-        for c in range(CHUNKS):
-            planes(c, *ys[c])
-            if c == CHUNKS - 2:
+            planes(c, ys[c])
+            if c == 1:
                 nc.sync.dma_start(out_words[:, : (c + 1) * CHUNK], y_words[:, : (c + 1) * CHUNK].bitcast(I32))
-        last = slice(S - CHUNK, S)
+        last = slice(2 * CHUNK, S)
         nc.sync.dma_start(out_words[:, last], y_words[:, last].bitcast(I32))
         for q in range(4):
             queue = nc.sync if q % 2 == 0 else nc.scalar

@@ -96,7 +96,7 @@ def tile_picked_zedge_silu_po_kernel(tc, x_words, x_scales, eT, w1, w2, w3, w4, 
             return words, scales
 
         w1_q = quantize_weight([(nc.scalar.copy, w1_raw[:], 0, ALL)], "w1", 1)
-        w2_q = quantize_weight([(nc.scalar.copy, w2_raw[:], 0, LOW), (nc.vector.tensor_copy, w2_raw[:], 0, HIGH)], "w2", 1)
+        w2_q = quantize_weight([(nc.scalar.copy, w2_raw[:], 0, LOW), (nc.vector.tensor_copy, w2_raw[:], 0, HIGH)], "w2", 2)
 
         def weave(dst_tile, src, copy=nc.vector.tensor_copy):
             copy(
@@ -117,13 +117,15 @@ def tile_picked_zedge_silu_po_kernel(tc, x_words, x_scales, eT, w1, w2, w3, w4, 
         quantize_edges(0, e_first[:], nc.scalar.copy)
         w3_q = quantize_weight(
             [
-                (nc.vector.tensor_copy, w3_raw[:], 0, LOW),
-                (nc.scalar.copy, w3_raw[:], 0, HIGH),
+                (nc.vector.tensor_copy, w3_raw[:, :, :336], 0, LOW),
+                (nc.scalar.copy, w3_raw[:, :, 336:], 84, LOW),
+                (nc.vector.tensor_copy, w3_raw[:, :, :176], 0, HIGH),
+                (nc.scalar.copy, w3_raw[:, :, 176:], 44, HIGH),
             ],
             "w3",
             4,
         )
-        quantize_edges(1, e_middle[:, :, :CHUNK], nc.scalar.copy)
+        quantize_edges(1, e_middle[:, :, :CHUNK], nc.vector.tensor_copy)
         quantize_edges(2, e_middle[:, :, CHUNK:], nc.scalar.copy)
         quantize_edges(3, e_last[:], nc.vector.tensor_copy)
 
@@ -178,9 +180,12 @@ def tile_picked_zedge_silu_po_kernel(tc, x_words, x_scales, eT, w1, w2, w3, w4, 
         out_rows = out_0.rearrange("(p t) n -> p t n", t=PACK)
         out_words = out_1[0].rearrange("p n t -> p (n t)").bitcast(I32)
 
-        def second_layer(c, shares):
+        def quantize_hidden(c):
             cols = slice(c * CHUNK, (c + 1) * CHUNK)
             nc.vector.quantize_mx(out=h_words[c].bitcast(FP8X4), scales=h_scales[:, cols], in_=hiddens[c][:])
+
+        def second_layer(c, shares):
+            cols = slice(c * CHUNK, (c + 1) * CHUNK)
             y = sb([P, PACK, CHUNK], F32, f"y{c}")
             for acc, slots, copy in shares:
                 for t in range(slots.start, slots.stop):
@@ -222,16 +227,20 @@ def tile_picked_zedge_silu_po_kernel(tc, x_words, x_scales, eT, w1, w2, w3, w4, 
         for c in range(CHUNKS):
             first_pass(c, 0, 1)
         quantize_w4_half(0, [(nc.vector.tensor_copy, w4_raw[0][:], 0, ALL)])
-        quantize_w4_half(1, [(nc.vector.tensor_copy, w4_raw[1][:], 0, ALL), (nc.vector.tensor_copy, w4_raw[2][:], 32, ALL)])
         h_first = sb([P, CHUNK], U32, "h_first", tag="w4_dealt0")
-        h_rest = sb([P, S - CHUNK], U32, "h_rest", tag="w4_dealt1")
-        h_words = [h_first[:]] + [h_rest[:, c * CHUNK : (c + 1) * CHUNK] for c in range(CHUNKS - 1)]
+        h_words = [h_first[:]]
         for c in range(CHUNKS):
             first_layer(c)
         spare = psum.tile([P, PACK, CHUNK], F32, name="spare", tag="pre0")
+        quantize_hidden(0)
+        quantize_w4_half(1, [(nc.vector.tensor_copy, w4_raw[1][:], 0, ALL), (nc.vector.tensor_copy, w4_raw[2][:], 32, ALL)])
+        h_rest = sb([P, S - CHUNK], U32, "h_rest", tag="w4_dealt1")
+        h_words.extend(h_rest[:, c * CHUNK : (c + 1) * CHUNK] for c in range(CHUNKS - 1))
         ys = [second_layer(0, [(accs[0], slice(0, 2), nc.vector.tensor_copy), (spare, slice(2, 4), nc.scalar.copy)])]
         for c in range(1, CHUNKS):
-            ys.append(second_layer(c, [(accs[c], slice(0, 4), nc.vector.tensor_copy if c == 1 else nc.scalar.copy)]))
+            quantize_hidden(c)
+        for c in range(1, CHUNKS):
+            ys.append(second_layer(c, [(accs[c], slice(0, 4), nc.vector.tensor_copy if c == 2 else nc.scalar.copy)]))
         for c in range(CHUNKS):
             planes(c, ys[c])
             if c == 1:

@@ -158,17 +158,15 @@ def tile_picked_zedge_silu_po_kernel(tc, x_words, x_scales, eT, w1, w2, w3, w4, 
                 lhsT_scale=stationary[g][1][:, rows],
                 rhs=moving[g][0][:, cols].bitcast(FP8X4),
                 rhs_scale=moving[g][1][:, cols],
-                start=(g == 0),
-                stop=(g == 2),
+                start=(g == 0 and t == 0),
+                stop=(g == 2 and t == PACK - 1),
             )
 
         hiddens = []
 
         def first_layer(c):
-            first_pass(c, 0, 2)
-            for t in range(1, PACK):
-                for g in range(3):
-                    first_pass(c, t, g)
+            for t in range(PACK):
+                first_pass(c, t, 2)
             hidden = sb([P, PACK * CHUNK], BF16, f"hidden{c}", tag="e_raw128" if c == 0 else None)
             hiddens.append(hidden)
             nc.scalar.activation(
@@ -184,9 +182,10 @@ def tile_picked_zedge_silu_po_kernel(tc, x_words, x_scales, eT, w1, w2, w3, w4, 
             cols = slice(c * CHUNK, (c + 1) * CHUNK)
             nc.vector.quantize_mx(out=h_words[c].bitcast(FP8X4), scales=h_scales[:, cols], in_=hiddens[c][:])
 
+        ys = [sb([P, PACK, CHUNK], F32, f"y{c}")[:] for c in range(CHUNKS)]
+
         def second_layer(c, shares):
             cols = slice(c * CHUNK, (c + 1) * CHUNK)
-            y = sb([P, PACK, CHUNK], F32, f"y{c}")
             for acc, slots, copy in shares:
                 for t in range(slots.start, slots.stop):
                     rows = slice(t * P, (t + 1) * P)
@@ -199,54 +198,88 @@ def tile_picked_zedge_silu_po_kernel(tc, x_words, x_scales, eT, w1, w2, w3, w4, 
                         start=True,
                         stop=True,
                     )
-                copy(y[:, slots], acc[:, slots])
-                nc.sync.dma_start(out_rows[:, slots, cols], y[:, slots])
-            return y
+                copy(ys[c][:, slots], acc[:, slots])
 
-        def planes(c, y):
-            cols = slice(c * CHUNK, (c + 1) * CHUNK)
+        def weave_result(c):
             woven = sb([P, PACK * CHUNK], BF16, f"y_woven{c}")
-            if c == CHUNKS - 1:
+            if c == 2:
                 nc.scalar.copy(woven[:].rearrange("p (n t) -> p n t", t=PACK), accs[c][:].rearrange("p t n -> p n t"))
             else:
-                weave(woven[:], y[:])
+                weave(woven[:], ys[c])
+            return woven
+
+        def store_result(c, slots):
+            nc.sync.dma_start(out_rows[:, slots, c * CHUNK : (c + 1) * CHUNK], ys[c][:, slots])
+
+        def quantize_result(c, woven):
+            cols = slice(c * CHUNK, (c + 1) * CHUNK)
             nc.vector.quantize_mx(out=y_words[:, cols].bitcast(FP8X4), scales=y_scales[:, cols], in_=woven[:])
 
-        for c in range(CHUNKS):
-            first_pass(c, 0, 0)
+        def early_passes(chunks):
+            for g in range(2):
+                for t in range(PACK):
+                    for c in chunks:
+                        first_pass(c, t, g)
+
+        early_passes(range(CHUNKS))
+        quantize_w4_half(0, [(nc.vector.tensor_copy, w4_raw[0][:], 0, ALL)])
+        for c in range(CHUNKS - 1):
+            first_layer(c)
+        dealt = sb([P, PACK, 64, PACK], BF16, "w4_dealt1")
+        deal(
+            dealt,
+            [
+                (nc.vector.tensor_copy, w4_raw[1][:], 0, ALL),
+                (nc.vector.tensor_copy, w4_raw[2][:], 32, ALL),
+            ],
+        )
+        first_layer(3)
         for i in range(6):
             nc.tensor.matmul_mx(
-                out=accs[i % CHUNKS][:, i // CHUNKS, :],
-                lhsT=w1_q[0][:, :P].bitcast(FP8X4),
-                lhsT_scale=w1_q[1][:, :P],
-                rhs=picked[0][0][:, :CHUNK].bitcast(FP8X4),
-                rhs_scale=picked[0][1][:, :CHUNK],
+                out=accs[3][:, i % PACK, :],
+                lhsT=w3_q[0][:, :P].bitcast(FP8X4),
+                lhsT_scale=w3_q[1][:, :P],
+                rhs=e_words[:, S - CHUNK :].bitcast(FP8X4),
+                rhs_scale=e_scales[:, S - CHUNK :],
                 start=True,
                 stop=True,
             )
-        for c in range(CHUNKS):
-            first_pass(c, 0, 1)
-        quantize_w4_half(0, [(nc.vector.tensor_copy, w4_raw[0][:], 0, ALL)])
-        h_first = sb([P, CHUNK], U32, "h_first", tag="w4_dealt0")
-        h_words = [h_first[:]]
-        for c in range(CHUNKS):
-            first_layer(c)
-        spare = psum.tile([P, PACK, CHUNK], F32, name="spare", tag="pre0")
+        h_first = sb([P, 2 * CHUNK], U32, "h_first", tag="w4_dealt0")
+        h_words = [h_first[:, :CHUNK], h_first[:, CHUNK:]]
         quantize_hidden(0)
-        quantize_w4_half(1, [(nc.vector.tensor_copy, w4_raw[1][:], 0, ALL), (nc.vector.tensor_copy, w4_raw[2][:], 32, ALL)])
-        h_rest = sb([P, S - CHUNK], U32, "h_rest", tag="w4_dealt1")
-        h_words.extend(h_rest[:, c * CHUNK : (c + 1) * CHUNK] for c in range(CHUNKS - 1))
-        ys = [second_layer(0, [(accs[0], slice(0, 2), nc.vector.tensor_copy), (spare, slice(2, 4), nc.scalar.copy)])]
-        for c in range(1, CHUNKS):
-            quantize_hidden(c)
-        for c in range(1, CHUNKS):
-            ys.append(second_layer(c, [(accs[c], slice(0, 4), nc.vector.tensor_copy if c == 2 else nc.scalar.copy)]))
-        for c in range(CHUNKS):
-            planes(c, ys[c])
-            if c == 1:
-                nc.sync.dma_start(out_words[:, : (c + 1) * CHUNK], y_words[:, : (c + 1) * CHUNK].bitcast(I32))
-        last = slice(2 * CHUNK, S)
-        nc.sync.dma_start(out_words[:, last], y_words[:, last].bitcast(I32))
+        quantize_hidden(1)
+        for t in range(PACK):
+            cols = slice(t * P + 64, (t + 1) * P)
+            nc.vector.quantize_mx(
+                out=w4_words[:, cols].bitcast(FP8X4),
+                scales=w4_scales[:, cols],
+                in_=dealt[:, t].rearrange("p m j -> p (m j)"),
+            )
+        h_rest = sb([P, 2 * CHUNK], U32, "h_rest", tag="w4_raw384")
+        h_words.extend([h_rest[:, :CHUNK], h_rest[:, CHUNK:]])
+        quantize_hidden(2)
+        quantize_hidden(3)
+        spares = [psum.tile([P, PACK, CHUNK], F32, name=f"spare{c}", tag=f"pre{c}") for c in range(3)]
+        low, high, whole = slice(0, 2), slice(2, PACK), slice(0, PACK)
+        second_layer(0, [(accs[0], low, nc.scalar.copy), (spares[0], high, nc.scalar.copy)])
+        store_result(0, low)
+        store_result(0, high)
+        second_layer(1, [(accs[1], low, nc.vector.tensor_copy), (spares[1], high, nc.scalar.copy)])
+        store_result(1, whole)
+        second_layer(2, [(accs[2], whole, nc.scalar.copy)])
+        store_result(2, whole)
+        y_woven = {0: weave_result(0)}
+        second_layer(3, [(accs[3], low, nc.vector.tensor_copy), (spares[2], high, nc.scalar.copy)])
+        store_result(3, whole)
+        y_woven[2] = weave_result(2)
+        y_woven[1] = weave_result(1)
+        quantize_result(0, y_woven[0])
+        y_woven[3] = weave_result(3)
+        quantize_result(1, y_woven[1])
+        quantize_result(2, y_woven[2])
+        nc.sync.dma_start(out_words[:, : 3 * CHUNK], y_words[:, : 3 * CHUNK].bitcast(I32))
+        quantize_result(3, y_woven[3])
+        nc.sync.dma_start(out_words[:, 3 * CHUNK :], y_words[:, 3 * CHUNK :].bitcast(I32))
         for q in range(4):
             queue = nc.sync if q % 2 == 0 else nc.scalar
             queue.dma_start(out_2[0, 4 * q : 4 * q + 4, :].bitcast(I32), y_scales[32 * q : 32 * q + 4, :].bitcast(I32))

@@ -145,7 +145,7 @@ def tile_picked_zedge_silu_po_kernel(tc, x_words, x_scales, eT, w1, w2, w3, w4, 
 
         moving = [picked[0], picked[1], [e_words, e_scales]]
         stationary = [w1_q, w2_q, w3_q]
-        pre = [psum.tile([P, PACK, CHUNK], F32, name=f"pre{c}") for c in range(CHUNKS)]
+        pre = [psum.tile([P, PACK, CHUNK], F32, name=f"pre{c}") for c in range(CHUNKS - 1)]
 
         accs = [psum.tile([P, PACK, CHUNK], F32, name=f"acc{c}") for c in range(CHUNKS)]
 
@@ -221,7 +221,18 @@ def tile_picked_zedge_silu_po_kernel(tc, x_words, x_scales, eT, w1, w2, w3, w4, 
                     for c in chunks:
                         first_pass(c, t, g)
 
-        early_passes(range(CHUNKS))
+        early_passes(range(CHUNKS - 1))
+        warm = psum.tile([P, PACK, CHUNK], F32, name="warm")
+        for i in range(5):
+            nc.tensor.matmul_mx(
+                out=warm[:, i % PACK, :],
+                lhsT=w3_q[0][:, :P].bitcast(FP8X4),
+                lhsT_scale=w3_q[1][:, :P],
+                rhs=picked[0][0][:, :CHUNK].bitcast(FP8X4),
+                rhs_scale=picked[0][1][:, :CHUNK],
+                start=True,
+                stop=True,
+            )
         quantize_w4_half(0, [(nc.vector.tensor_copy, w4_raw[0][:], 0, ALL)])
         for c in range(CHUNKS - 1):
             first_layer(c)
@@ -233,17 +244,9 @@ def tile_picked_zedge_silu_po_kernel(tc, x_words, x_scales, eT, w1, w2, w3, w4, 
                 (nc.vector.tensor_copy, w4_raw[2][:], 32, ALL),
             ],
         )
+        pre.append(psum.tile([P, PACK, CHUNK], F32, name="pre3", tag="pre0"))
+        early_passes((3,))
         first_layer(3)
-        for i in range(6):
-            nc.tensor.matmul_mx(
-                out=accs[3][:, i % PACK, :],
-                lhsT=w3_q[0][:, :P].bitcast(FP8X4),
-                lhsT_scale=w3_q[1][:, :P],
-                rhs=e_words[:, S - CHUNK :].bitcast(FP8X4),
-                rhs_scale=e_scales[:, S - CHUNK :],
-                start=True,
-                stop=True,
-            )
         h_first = sb([P, 2 * CHUNK], U32, "h_first", tag="w4_dealt0")
         h_words = [h_first[:, :CHUNK], h_first[:, CHUNK:]]
         quantize_hidden(0)
@@ -259,7 +262,7 @@ def tile_picked_zedge_silu_po_kernel(tc, x_words, x_scales, eT, w1, w2, w3, w4, 
         h_words.extend([h_rest[:, :CHUNK], h_rest[:, CHUNK:]])
         quantize_hidden(2)
         quantize_hidden(3)
-        spares = [psum.tile([P, PACK, CHUNK], F32, name=f"spare{c}", tag=f"pre{c}") for c in range(3)]
+        spares = [psum.tile([P, PACK, CHUNK], F32, name=f"spare{c}", tag=("warm", "pre1", "pre2")[c]) for c in range(3)]
         low, high, whole = slice(0, 2), slice(2, PACK), slice(0, PACK)
         second_layer(0, [(accs[0], low, nc.scalar.copy), (spares[0], high, nc.scalar.copy)])
         store_result(0, low)

@@ -18,7 +18,6 @@ P = 128
 PACK = 4
 CHUNK = 128
 CHUNKS = S // CHUNK
-ALL, LOW, HIGH = slice(0, 2), slice(0, 1), slice(1, 2)
 
 
 def tile_picked_zedge_silu_po_kernel(tc, x_words, x_scales, eT, w1, w2, w3, w4, offs, dst, out_0, out_1, out_2):
@@ -55,11 +54,9 @@ def tile_picked_zedge_silu_po_kernel(tc, x_words, x_scales, eT, w1, w2, w3, w4, 
 
         w1_raw = load(w1, "w1", 0, H)
         w2_raw = load(w2, "w2", 0, H)
-        e_first = load(eT, "e", 0, CHUNK)
         w3_raw = load(w3, "w3", 0, H)
-        e_middle = load(eT, "e", CHUNK, 2 * CHUNK)
-        e_last = load(eT, "e", 3 * CHUNK, CHUNK)
-        w4_raw = [load(w4, "w4", 0, 256), load(w4, "w4", 256, 128), load(w4, "w4", 384, 128)]
+        e_raw = load(eT, "e", 0, S)
+        w4_raw = [load(w4, "w4", 0, N // 2), load(w4, "w4", N // 2, N // 2)]
 
         picked = []
         for name, offsets in (("sender", senders), ("receiver", receivers)):
@@ -71,32 +68,29 @@ def tile_picked_zedge_silu_po_kernel(tc, x_words, x_scales, eT, w1, w2, w3, w4, 
             nc.vector.tensor_copy(scales[:], node_scales[:].indirect(offsets[:]))
             picked[i].append(scales)
 
-        def deal(dealt, parts):
-            for copy, src, first, slots in parts:
-                count = src.shape[2] // PACK
-                copy(
-                    dealt[:].rearrange("p (u v) m j -> p u m j v", v=2)[:, slots, first : first + count],
-                    src.rearrange("p j (m u v) -> p u m j v", u=2, v=2)[:, slots],
-                )
+        def deal(copy, src, name):
+            dealt = sb([P, 2, src.shape[1], PACK], BF16, name)
+            copy(dealt[:].rearrange("p v m j -> p m j v"), src)
+            return dealt
 
-        def quantize_weight(parts, name, calls):
-            dealt = sb([P, PACK, P, PACK], BF16, name + "_dealt")
-            deal(dealt, parts)
-            flat = dealt[:].rearrange("p t m j -> p (t m j)")
-            words = sb([P, H], U32, name + "_words")
-            scales = sb([P, H], U8, name + "_scales")
-            width = H // calls
-            for c in range(calls):
-                cols = slice(c * width, (c + 1) * width)
-                nc.vector.quantize_mx(
-                    out=words[:, cols].bitcast(FP8X4),
-                    scales=scales[:, cols],
-                    in_=flat[:, PACK * c * width : PACK * (c + 1) * width],
-                )
+        def pair(raw, u):
+            return raw[:].rearrange("p j (m u v) -> p u m j v", u=2, v=2)[:, u]
+
+        def quantize_pair(dealt, name, tag=None):
+            words = sb([P, 2 * P], U32, name + "_words", tag=tag)
+            scales = sb([P, 2 * P], U8, name + "_scales")
+            nc.vector.quantize_mx(
+                out=words[:].bitcast(FP8X4), scales=scales[:], in_=dealt[:].rearrange("p v m j -> p (v m j)")
+            )
             return words, scales
 
-        w1_q = quantize_weight([(nc.scalar.copy, w1_raw[:], 0, ALL)], "w1", 1)
-        w2_q = quantize_weight([(nc.scalar.copy, w2_raw[:], 0, LOW), (nc.vector.tensor_copy, w2_raw[:], 0, HIGH)], "w2", 2)
+        w1_dealt = [deal(nc.scalar.copy, pair(w1_raw, u), f"w1_dealt{u}") for u in range(2)]
+        w1_q = [quantize_pair(w1_dealt[u], f"w1_{u}") for u in range(2)]
+        w2_dealt = [deal(nc.scalar.copy, pair(w2_raw, 0), "w2_dealt0"), deal(nc.vector.tensor_copy, pair(w2_raw, 1), "w2_dealt1")]
+        w2_q = [quantize_pair(w2_dealt[0], "w2_0")]
+        w3_dealt = [deal(nc.vector.tensor_copy, pair(w3_raw, 0), "w3_dealt0"), deal(nc.scalar.copy, pair(w3_raw, 1), "w3_dealt1")]
+        w3_q = [quantize_pair(w3_dealt[u], f"w3_{u}") for u in range(2)]
+        w2_q.append(quantize_pair(w2_dealt[1], "w2_1", tag="w3_raw0"))
 
         def weave(dst_tile, src, copy=nc.vector.tensor_copy):
             copy(
@@ -108,39 +102,41 @@ def tile_picked_zedge_silu_po_kernel(tc, x_words, x_scales, eT, w1, w2, w3, w4, 
         e_scales = sb([P, S], U8, "e_scales")
         h_scales = sb([P, S], U8, "h_scales")
 
-        def quantize_edges(c, src, copy):
-            cols = slice(c * CHUNK, (c + 1) * CHUNK)
-            woven = sb([P, PACK * CHUNK], BF16, f"e_woven{c}")
-            weave(woven[:], src, copy)
-            nc.vector.quantize_mx(out=e_words[:, cols].bitcast(FP8X4), scales=e_scales[:, cols], in_=woven[:])
+        e_woven = [sb([P, PACK * CHUNK], BF16, f"e_woven{c}") for c in range(CHUNKS)]
 
-        quantize_edges(0, e_first[:], nc.scalar.copy)
-        w3_q = quantize_weight(
-            [
-                (nc.vector.tensor_copy, w3_raw[:, :, :336], 0, LOW),
-                (nc.scalar.copy, w3_raw[:, :, 336:], 84, LOW),
-                (nc.vector.tensor_copy, w3_raw[:, :, :176], 0, HIGH),
-                (nc.scalar.copy, w3_raw[:, :, 176:], 44, HIGH),
-            ],
-            "w3",
-            4,
-        )
-        quantize_edges(1, e_middle[:, :, :CHUNK], nc.vector.tensor_copy)
-        quantize_edges(2, e_middle[:, :, CHUNK:], nc.scalar.copy)
-        quantize_edges(3, e_last[:], nc.vector.tensor_copy)
+        def weave_edges(c, first, count, copy):
+            weave(
+                e_woven[c][:, PACK * first : PACK * (first + count)],
+                e_raw[:, :, c * CHUNK + first : c * CHUNK + first + count],
+                copy,
+            )
+
+        def quantize_edges(c):
+            cols = slice(c * CHUNK, (c + 1) * CHUNK)
+            nc.vector.quantize_mx(out=e_words[:, cols].bitcast(FP8X4), scales=e_scales[:, cols], in_=e_woven[c][:])
+
+        half = CHUNK // 2
+        weave_edges(0, 0, half, nc.vector.tensor_copy)
+        weave_edges(0, half, half, nc.scalar.copy)
+        weave_edges(1, 0, CHUNK, nc.vector.tensor_copy)
+        weave_edges(2, 0, CHUNK, nc.scalar.copy)
+        quantize_edges(0)
+        weave_edges(3, 0, half, nc.vector.tensor_copy)
+        weave_edges(3, half, half, nc.scalar.copy)
+        for c in range(1, CHUNKS):
+            quantize_edges(c)
 
         w4_words = sb([P, N], U32, "w4_words")
         w4_scales = sb([P, N], U8, "w4_scales")
 
-        def quantize_w4_half(half, parts):
-            dealt = sb([P, PACK, 64, PACK], BF16, f"w4_dealt{half}")
-            deal(dealt, parts)
-            for t in range(PACK):
-                cols = slice(t * P + half * 64, t * P + (half + 1) * 64)
+        def quantize_w4(half, u, dealt):
+            for v in range(2):
+                first = (2 * u + v) * P + half * 64
+                cols = slice(first, first + 64)
                 nc.vector.quantize_mx(
                     out=w4_words[:, cols].bitcast(FP8X4),
                     scales=w4_scales[:, cols],
-                    in_=dealt[:, t].rearrange("p m j -> p (m j)"),
+                    in_=dealt[:, v].rearrange("p m j -> p (m j)"),
                 )
 
         moving = [picked[0], picked[1], [e_words, e_scales]]
@@ -151,11 +147,11 @@ def tile_picked_zedge_silu_po_kernel(tc, x_words, x_scales, eT, w1, w2, w3, w4, 
 
         def first_pass(c, t, g):
             cols = slice(c * CHUNK, (c + 1) * CHUNK)
-            rows = slice(t * P, (t + 1) * P)
+            rows = slice(t % 2 * P, (t % 2 + 1) * P)
             nc.tensor.matmul_mx(
                 out=pre[c][:, t, :],
-                lhsT=stationary[g][0][:, rows].bitcast(FP8X4),
-                lhsT_scale=stationary[g][1][:, rows],
+                lhsT=stationary[g][t // 2][0][:, rows].bitcast(FP8X4),
+                lhsT_scale=stationary[g][t // 2][1][:, rows],
                 rhs=moving[g][0][:, cols].bitcast(FP8X4),
                 rhs_scale=moving[g][1][:, cols],
                 start=(g == 0 and t == 0),
@@ -167,7 +163,7 @@ def tile_picked_zedge_silu_po_kernel(tc, x_words, x_scales, eT, w1, w2, w3, w4, 
         def first_layer(c):
             for t in range(PACK):
                 first_pass(c, t, 2)
-            hidden = sb([P, PACK * CHUNK], BF16, f"hidden{c}", tag="e_raw128" if c == 0 else None)
+            hidden = sb([P, PACK * CHUNK], BF16, f"hidden{c}")
             hiddens.append(hidden)
             nc.scalar.activation(
                 hidden[:].rearrange("p (n t) -> p n t", t=PACK), pre[c][:].rearrange("p t n -> p n t"), SILU
@@ -222,47 +218,25 @@ def tile_picked_zedge_silu_po_kernel(tc, x_words, x_scales, eT, w1, w2, w3, w4, 
                         first_pass(c, t, g)
 
         early_passes(range(CHUNKS - 1))
-        warm = psum.tile([P, PACK, CHUNK], F32, name="warm")
-        for i in range(5):
-            nc.tensor.matmul_mx(
-                out=warm[:, i % PACK, :],
-                lhsT=w3_q[0][:, :P].bitcast(FP8X4),
-                lhsT_scale=w3_q[1][:, :P],
-                rhs=picked[0][0][:, :CHUNK].bitcast(FP8X4),
-                rhs_scale=picked[0][1][:, :CHUNK],
-                start=True,
-                stop=True,
-            )
-        quantize_w4_half(0, [(nc.vector.tensor_copy, w4_raw[0][:], 0, ALL)])
         for c in range(CHUNKS - 1):
             first_layer(c)
-        dealt = sb([P, PACK, 64, PACK], BF16, "w4_dealt1")
-        deal(
-            dealt,
-            [
-                (nc.vector.tensor_copy, w4_raw[1][:], 0, ALL),
-                (nc.vector.tensor_copy, w4_raw[2][:], 32, ALL),
-            ],
-        )
         pre.append(psum.tile([P, PACK, CHUNK], F32, name="pre3", tag="pre0"))
         early_passes((3,))
         first_layer(3)
-        h_first = sb([P, 2 * CHUNK], U32, "h_first", tag="w4_dealt0")
-        h_words = [h_first[:, :CHUNK], h_first[:, CHUNK:]]
+        w4_dealt = [deal(nc.vector.tensor_copy, pair(w4_raw[0], u), f"w4_dealt0{u}") for u in range(2)]
+        for u in range(2):
+            quantize_w4(0, u, w4_dealt[u])
+        h_words = [sb([P, CHUNK], U32, "h_first", tag="w4_dealt00")[:]]
         quantize_hidden(0)
+        w4_dealt = [deal(nc.vector.tensor_copy, pair(w4_raw[1], u), f"w4_dealt1{u}") for u in range(2)]
+        quantize_w4(1, 0, w4_dealt[0])
+        h_rest = sb([P, S - CHUNK], U32, "h_rest", tag="w4_raw256")
+        h_words.extend(h_rest[:, c * CHUNK : (c + 1) * CHUNK] for c in range(CHUNKS - 1))
         quantize_hidden(1)
-        for t in range(PACK):
-            cols = slice(t * P + 64, (t + 1) * P)
-            nc.vector.quantize_mx(
-                out=w4_words[:, cols].bitcast(FP8X4),
-                scales=w4_scales[:, cols],
-                in_=dealt[:, t].rearrange("p m j -> p (m j)"),
-            )
-        h_rest = sb([P, 2 * CHUNK], U32, "h_rest", tag="w4_raw384")
-        h_words.extend([h_rest[:, :CHUNK], h_rest[:, CHUNK:]])
+        quantize_w4(1, 1, w4_dealt[1])
         quantize_hidden(2)
         quantize_hidden(3)
-        spares = [psum.tile([P, PACK, CHUNK], F32, name=f"spare{c}", tag=("warm", "pre1", "pre2")[c]) for c in range(3)]
+        spares = [psum.tile([P, PACK, CHUNK], F32, name=f"spare{c}", tag=("spare0", "pre1", "pre2")[c]) for c in range(3)]
         low, high, whole = slice(0, 2), slice(2, PACK), slice(0, PACK)
         second_layer(0, [(accs[0], low, nc.scalar.copy), (spares[0], high, nc.scalar.copy)])
         store_result(0, low)

@@ -18,6 +18,8 @@ P = 128
 PACK = 4
 CHUNK = 128
 CHUNKS = S // CHUNK
+LAST = CHUNKS - 1
+SENDER, RECEIVER, EDGE = 0, 1, 2
 
 
 def tile_picked_zedge_silu_po_kernel(tc, x_words, x_scales, eT, w1, w2, w3, w4, offs, dst, out_0, out_1, out_2):
@@ -68,13 +70,13 @@ def tile_picked_zedge_silu_po_kernel(tc, x_words, x_scales, eT, w1, w2, w3, w4, 
             nc.vector.tensor_copy(scales[:], node_scales[:].indirect(offsets[:]))
             picked[i].append(scales)
 
-        def deal(copy, src, name):
-            dealt = sb([P, 2, src.shape[1], PACK], BF16, name)
-            copy(dealt[:].rearrange("p v m j -> p m j v"), src)
-            return dealt
-
         def pair(raw, u):
             return raw[:].rearrange("p j (m u v) -> p u m j v", u=2, v=2)[:, u]
+
+        def deal(copy, src, name, tag=None):
+            dealt = sb([P, 2, src.shape[1], PACK], BF16, name, tag=tag)
+            copy(dealt[:].rearrange("p v m j -> p m j v"), src)
+            return dealt
 
         def quantize_pair(dealt, name, tag=None):
             words = sb([P, 2 * P], U32, name + "_words", tag=tag)
@@ -101,7 +103,6 @@ def tile_picked_zedge_silu_po_kernel(tc, x_words, x_scales, eT, w1, w2, w3, w4, 
         e_words = sb([P, S], U32, "e_words")
         e_scales = sb([P, S], U8, "e_scales")
         h_scales = sb([P, S], U8, "h_scales")
-
         e_woven = [sb([P, PACK * CHUNK], BF16, f"e_woven{c}") for c in range(CHUNKS)]
 
         def weave_edges(c, first, count, copy):
@@ -115,14 +116,13 @@ def tile_picked_zedge_silu_po_kernel(tc, x_words, x_scales, eT, w1, w2, w3, w4, 
             cols = slice(c * CHUNK, (c + 1) * CHUNK)
             nc.vector.quantize_mx(out=e_words[:, cols].bitcast(FP8X4), scales=e_scales[:, cols], in_=e_woven[c][:])
 
-        half = CHUNK // 2
-        weave_edges(0, 0, half, nc.vector.tensor_copy)
-        weave_edges(0, half, half, nc.scalar.copy)
+        half_chunk = CHUNK // 2
+        weave_edges(0, 0, half_chunk, nc.vector.tensor_copy)
+        weave_edges(0, half_chunk, half_chunk, nc.scalar.copy)
         weave_edges(1, 0, CHUNK, nc.vector.tensor_copy)
         weave_edges(2, 0, CHUNK, nc.scalar.copy)
         quantize_edges(0)
-        weave_edges(3, 0, half, nc.vector.tensor_copy)
-        weave_edges(3, half, half, nc.scalar.copy)
+        weave_edges(3, 0, CHUNK, nc.scalar.copy)
         for c in range(1, CHUNKS):
             quantize_edges(c)
 
@@ -131,8 +131,8 @@ def tile_picked_zedge_silu_po_kernel(tc, x_words, x_scales, eT, w1, w2, w3, w4, 
 
         def quantize_w4(half, u, dealt):
             for v in range(2):
-                first = (2 * u + v) * P + half * 64
-                cols = slice(first, first + 64)
+                first = (2 * u + v) * P + half * (P // 2)
+                cols = slice(first, first + P // 2)
                 nc.vector.quantize_mx(
                     out=w4_words[:, cols].bitcast(FP8X4),
                     scales=w4_scales[:, cols],
@@ -141,9 +141,8 @@ def tile_picked_zedge_silu_po_kernel(tc, x_words, x_scales, eT, w1, w2, w3, w4, 
 
         moving = [picked[0], picked[1], [e_words, e_scales]]
         stationary = [w1_q, w2_q, w3_q]
-        pre = [psum.tile([P, PACK, CHUNK], F32, name=f"pre{c}") for c in range(CHUNKS - 1)]
-
-        accs = [psum.tile([P, PACK, CHUNK], F32, name=f"acc{c}") for c in range(CHUNKS)]
+        pre = [psum.tile([P, PACK, CHUNK], F32, name=f"pre{c}") for c in range(CHUNKS)]
+        accs = [psum.tile([P, PACK, CHUNK], F32, name=f"acc{c}") for c in range(LAST)]
 
         def first_pass(c, t, g):
             cols = slice(c * CHUNK, (c + 1) * CHUNK)
@@ -154,15 +153,16 @@ def tile_picked_zedge_silu_po_kernel(tc, x_words, x_scales, eT, w1, w2, w3, w4, 
                 lhsT_scale=stationary[g][t // 2][1][:, rows],
                 rhs=moving[g][0][:, cols].bitcast(FP8X4),
                 rhs_scale=moving[g][1][:, cols],
-                start=(g == 0 and t == 0),
-                stop=(g == 2 and t == PACK - 1),
+                start=(g == SENDER and t == 0),
+                stop=(g == (RECEIVER if c == LAST else EDGE) and t == PACK - 1),
             )
 
         hiddens = []
 
         def first_layer(c):
-            for t in range(PACK):
-                first_pass(c, t, 2)
+            for g in (EDGE, RECEIVER) if c == LAST else (EDGE,):
+                for t in range(PACK):
+                    first_pass(c, t, g)
             hidden = sb([P, PACK * CHUNK], BF16, f"hidden{c}")
             hiddens.append(hidden)
             nc.scalar.activation(
@@ -182,8 +182,8 @@ def tile_picked_zedge_silu_po_kernel(tc, x_words, x_scales, eT, w1, w2, w3, w4, 
 
         def second_layer(c, shares):
             cols = slice(c * CHUNK, (c + 1) * CHUNK)
-            for acc, slots, copy in shares:
-                for t in range(slots.start, slots.stop):
+            for acc, slices, copy in shares:
+                for t in range(slices.start, slices.stop):
                     rows = slice(t * P, (t + 1) * P)
                     nc.tensor.matmul_mx(
                         out=acc[:, t, :],
@@ -194,49 +194,49 @@ def tile_picked_zedge_silu_po_kernel(tc, x_words, x_scales, eT, w1, w2, w3, w4, 
                         start=True,
                         stop=True,
                     )
-                copy(ys[c][:, slots], acc[:, slots])
+                copy(ys[c][:, slices], acc[:, slices])
 
         def weave_result(c):
             woven = sb([P, PACK * CHUNK], BF16, f"y_woven{c}")
-            if c == 2:
-                nc.scalar.copy(woven[:].rearrange("p (n t) -> p n t", t=PACK), accs[c][:].rearrange("p t n -> p n t"))
-            else:
-                weave(woven[:], ys[c])
+            weave(woven[:], ys[c])
             return woven
 
-        def store_result(c, slots):
-            nc.sync.dma_start(out_rows[:, slots, c * CHUNK : (c + 1) * CHUNK], ys[c][:, slots])
+        def weave_result_from_bank(c):
+            woven = sb([P, PACK * CHUNK], BF16, f"y_woven{c}")
+            nc.scalar.copy(woven[:].rearrange("p (n t) -> p n t", t=PACK), accs[c][:].rearrange("p t n -> p n t"))
+            return woven
+
+        def store_result(c, slices):
+            nc.sync.dma_start(out_rows[:, slices, c * CHUNK : (c + 1) * CHUNK], ys[c][:, slices])
 
         def quantize_result(c, woven):
             cols = slice(c * CHUNK, (c + 1) * CHUNK)
             nc.vector.quantize_mx(out=y_words[:, cols].bitcast(FP8X4), scales=y_scales[:, cols], in_=woven[:])
 
-        def early_passes(chunks):
-            for g in range(2):
-                for t in range(PACK):
-                    for c in chunks:
-                        first_pass(c, t, g)
-
-        early_passes(range(CHUNKS - 1))
-        for c in range(CHUNKS - 1):
+        for g, chunks in ((SENDER, CHUNKS), (RECEIVER, LAST)):
+            for t in range(PACK):
+                for c in range(chunks):
+                    first_pass(c, t, g)
+        for c in range(CHUNKS):
             first_layer(c)
-        pre.append(psum.tile([P, PACK, CHUNK], F32, name="pre3", tag="pre0"))
-        early_passes((3,))
-        first_layer(3)
-        w4_dealt = [deal(nc.vector.tensor_copy, pair(w4_raw[0], u), f"w4_dealt0{u}") for u in range(2)]
+
+        w4_first = [deal(nc.vector.tensor_copy, pair(w4_raw[0], u), f"w4_dealt0{u}") for u in range(2)]
         for u in range(2):
-            quantize_w4(0, u, w4_dealt[u])
+            quantize_w4(0, u, w4_first[u])
         h_words = [sb([P, CHUNK], U32, "h_first", tag="w4_dealt00")[:]]
         quantize_hidden(0)
-        w4_dealt = [deal(nc.vector.tensor_copy, pair(w4_raw[1], u), f"w4_dealt1{u}") for u in range(2)]
-        quantize_w4(1, 0, w4_dealt[0])
+        w4_second = [
+            deal(nc.vector.tensor_copy, pair(w4_raw[1], u), f"w4_dealt1{u}", tag=("w4_dealt01", "hidden0")[u]) for u in range(2)
+        ]
+        for u in range(2):
+            quantize_w4(1, u, w4_second[u])
         h_rest = sb([P, S - CHUNK], U32, "h_rest", tag="w4_raw256")
-        h_words.extend(h_rest[:, c * CHUNK : (c + 1) * CHUNK] for c in range(CHUNKS - 1))
-        quantize_hidden(1)
-        quantize_w4(1, 1, w4_dealt[1])
-        quantize_hidden(2)
-        quantize_hidden(3)
-        spares = [psum.tile([P, PACK, CHUNK], F32, name=f"spare{c}", tag=("spare0", "pre1", "pre2")[c]) for c in range(3)]
+        h_words.extend(h_rest[:, c * CHUNK : (c + 1) * CHUNK] for c in range(LAST))
+        for c in range(1, CHUNKS):
+            quantize_hidden(c)
+
+        accs.append(psum.tile([P, PACK, CHUNK], F32, name="acc3", tag="pre1"))
+        spares = [psum.tile([P, PACK, CHUNK], F32, name=f"spare{i}", tag=("spare0", "pre0", "pre2")[i]) for i in range(3)]
         low, high, whole = slice(0, 2), slice(2, PACK), slice(0, PACK)
         second_layer(0, [(accs[0], low, nc.scalar.copy), (spares[0], high, nc.scalar.copy)])
         store_result(0, low)
@@ -248,15 +248,16 @@ def tile_picked_zedge_silu_po_kernel(tc, x_words, x_scales, eT, w1, w2, w3, w4, 
         y_woven = {0: weave_result(0)}
         second_layer(3, [(accs[3], low, nc.vector.tensor_copy), (spares[2], high, nc.scalar.copy)])
         store_result(3, whole)
-        y_woven[2] = weave_result(2)
+
+        y_woven[2] = weave_result_from_bank(2)
         y_woven[1] = weave_result(1)
         quantize_result(0, y_woven[0])
         y_woven[3] = weave_result(3)
         quantize_result(1, y_woven[1])
         quantize_result(2, y_woven[2])
-        nc.sync.dma_start(out_words[:, : 3 * CHUNK], y_words[:, : 3 * CHUNK].bitcast(I32))
+        nc.sync.dma_start(out_words[:, : LAST * CHUNK], y_words[:, : LAST * CHUNK].bitcast(I32))
         quantize_result(3, y_woven[3])
-        nc.sync.dma_start(out_words[:, 3 * CHUNK :], y_words[:, 3 * CHUNK :].bitcast(I32))
+        nc.sync.dma_start(out_words[:, LAST * CHUNK :], y_words[:, LAST * CHUNK :].bitcast(I32))
         for q in range(4):
             queue = nc.sync if q % 2 == 0 else nc.scalar
             queue.dma_start(out_2[0, 4 * q : 4 * q + 4, :].bitcast(I32), y_scales[32 * q : 32 * q + 4, :].bitcast(I32))

@@ -47,7 +47,7 @@ def tile_picked_zedge_silu_po_kernel(tc, x_words, x_scales, eT, w1, w2, w3, w4, 
         nc.sync.dma_start(senders[:], offs)
         nc.sync.dma_start(receivers[:], dst)
         for q in range(4):
-            nc.sync.dma_start(node_scales[32 * q : 32 * q + 4, :].bitcast(I32), x_scales[0, 4 * q : 4 * q + 4, :].bitcast(I32))
+            nc.scalar.dma_start(node_scales[32 * q : 32 * q + 4, :].bitcast(I32), x_scales[0, 4 * q : 4 * q + 4, :].bitcast(I32))
 
         def load(w, name, first, width):
             raw = sb([P, PACK, width], F32, f"{name}_raw{first}")

@@ -19,6 +19,7 @@ PACK = 4
 CHUNK = 128
 CHUNKS = S // CHUNK
 LAST = CHUNKS - 1
+HALF = S // 2
 SENDER, RECEIVER, EDGE = 0, 1, 2
 
 
@@ -33,11 +34,11 @@ def tile_picked_zedge_silu_po_kernel(tc, x_words, x_scales, eT, w1, w2, w3, w4, 
             return keep.tile(shape, dtype, name=name, tag=tag or name, align_bytes=64)
 
         node_scales = sb([P, T], U8, "node_scales")
-        nc.vector.memset(node_scales[:].bitcast(I32), 0)
+        nc.gpsimd.memset(node_scales[:].bitcast(I32), 0)
 
         warm_in = sb([P, 1], F32, "warm_in")
         warm_out = sb([P, 1], F32, "warm_out")
-        nc.vector.memset(warm_in[:], 0.0)
+        nc.gpsimd.memset(warm_in[:], 0.0)
         nc.scalar.activation(warm_out[:], warm_in[:], SILU)
 
         node_words = sb([P, T], U32, "node_words")
@@ -142,7 +143,6 @@ def tile_picked_zedge_silu_po_kernel(tc, x_words, x_scales, eT, w1, w2, w3, w4, 
         moving = [picked[0], picked[1], [e_words, e_scales]]
         stationary = [w1_q, w2_q, w3_q]
         pre = [psum.tile([P, PACK, CHUNK], F32, name=f"pre{c}") for c in range(CHUNKS)]
-        accs = [psum.tile([P, PACK, CHUNK], F32, name=f"acc{c}") for c in range(LAST)]
 
         def first_pass(c, t, g):
             cols = slice(c * CHUNK, (c + 1) * CHUNK)
@@ -176,38 +176,35 @@ def tile_picked_zedge_silu_po_kernel(tc, x_words, x_scales, eT, w1, w2, w3, w4, 
 
         def quantize_hidden(c):
             cols = slice(c * CHUNK, (c + 1) * CHUNK)
-            nc.vector.quantize_mx(out=h_words[c].bitcast(FP8X4), scales=h_scales[:, cols], in_=hiddens[c][:])
+            words = h_words[c // 2][:, c % 2 * CHUNK : (c % 2 + 1) * CHUNK]
+            nc.vector.quantize_mx(out=words.bitcast(FP8X4), scales=h_scales[:, cols], in_=hiddens[c][:])
 
-        ys = [sb([P, PACK, CHUNK], F32, f"y{c}")[:] for c in range(CHUNKS)]
+        ys = [sb([P, PACK, HALF], F32, f"y{b}") for b in range(2)]
 
-        def second_layer(c, shares):
-            cols = slice(c * CHUNK, (c + 1) * CHUNK)
-            for acc, slices, copy in shares:
-                for t in range(slices.start, slices.stop):
-                    rows = slice(t * P, (t + 1) * P)
-                    nc.tensor.matmul_mx(
-                        out=acc[:, t, :],
-                        lhsT=w4_words[:, rows].bitcast(FP8X4),
-                        lhsT_scale=w4_scales[:, rows],
-                        rhs=h_words[c].bitcast(FP8X4),
-                        rhs_scale=h_scales[:, cols],
-                        start=True,
-                        stop=True,
-                    )
-                copy(ys[c][:, slices], acc[:, slices])
+        def second_layer(b, t, copy):
+            acc = psum.tile([P, HALF], F32, name=f"acc{b}{t}", tag=f"pre{t}" if b else f"acc{t}")
+            rows = slice(t * P, (t + 1) * P)
+            nc.tensor.matmul_mx(
+                out=acc[:],
+                lhsT=w4_words[:, rows].bitcast(FP8X4),
+                lhsT_scale=w4_scales[:, rows],
+                rhs=h_words[b][:].bitcast(FP8X4),
+                rhs_scale=h_scales[:, b * HALF : (b + 1) * HALF],
+                start=True,
+                stop=True,
+            )
+            copy(ys[b][:, t], acc[:])
 
-        def weave_result(c):
+        def result_chunk(c):
+            return ys[c // 2][:, :, c % 2 * CHUNK : (c % 2 + 1) * CHUNK]
+
+        def weave_result(c, copy):
             woven = sb([P, PACK * CHUNK], BF16, f"y_woven{c}")
-            weave(woven[:], ys[c])
+            weave(woven[:], result_chunk(c), copy)
             return woven
 
-        def weave_result_from_bank(c):
-            woven = sb([P, PACK * CHUNK], BF16, f"y_woven{c}")
-            nc.scalar.copy(woven[:].rearrange("p (n t) -> p n t", t=PACK), accs[c][:].rearrange("p t n -> p n t"))
-            return woven
-
-        def store_result(c, slices):
-            nc.sync.dma_start(out_rows[:, slices, c * CHUNK : (c + 1) * CHUNK], ys[c][:, slices])
+        def store_result(b, slices):
+            nc.sync.dma_start(out_rows[:, slices, b * HALF : (b + 1) * HALF], ys[b][:, slices])
 
         def quantize_result(c, woven):
             cols = slice(c * CHUNK, (c + 1) * CHUNK)
@@ -223,40 +220,37 @@ def tile_picked_zedge_silu_po_kernel(tc, x_words, x_scales, eT, w1, w2, w3, w4, 
         w4_first = [deal(nc.vector.tensor_copy, pair(w4_raw[0], u), f"w4_dealt0{u}") for u in range(2)]
         for u in range(2):
             quantize_w4(0, u, w4_first[u])
-        h_words = [sb([P, CHUNK], U32, "h_first", tag="w4_dealt00")[:]]
+        h_words = [sb([P, HALF], U32, "h_first", tag="w4_dealt00")]
         quantize_hidden(0)
         w4_second = [
             deal(nc.vector.tensor_copy, pair(w4_raw[1], u), f"w4_dealt1{u}", tag=("w4_dealt01", "hidden0")[u]) for u in range(2)
         ]
+        quantize_hidden(1)
         for u in range(2):
             quantize_w4(1, u, w4_second[u])
-        h_rest = sb([P, S - CHUNK], U32, "h_rest", tag="w4_raw256")
-        h_words.extend(h_rest[:, c * CHUNK : (c + 1) * CHUNK] for c in range(LAST))
-        for c in range(1, CHUNKS):
-            quantize_hidden(c)
+        h_words.append(sb([P, HALF], U32, "h_rest", tag="w4_raw256"))
+        quantize_hidden(2)
+        quantize_hidden(3)
 
-        accs.append(psum.tile([P, PACK, CHUNK], F32, name="acc3", tag="pre1"))
-        spares = [psum.tile([P, PACK, CHUNK], F32, name=f"spare{i}", tag=("spare0", "pre0", "pre2")[i]) for i in range(3)]
-        low, high, whole = slice(0, 2), slice(2, PACK), slice(0, PACK)
-        second_layer(0, [(accs[0], low, nc.scalar.copy), (spares[0], high, nc.scalar.copy)])
-        store_result(0, low)
-        store_result(0, high)
-        second_layer(1, [(accs[1], low, nc.vector.tensor_copy), (spares[1], high, nc.scalar.copy)])
-        store_result(1, whole)
-        second_layer(2, [(accs[2], whole, nc.scalar.copy)])
-        store_result(2, whole)
-        y_woven = {0: weave_result(0)}
-        second_layer(3, [(accs[3], low, nc.vector.tensor_copy), (spares[2], high, nc.scalar.copy)])
-        store_result(3, whole)
-
-        y_woven[2] = weave_result_from_bank(2)
-        y_woven[1] = weave_result(1)
-        quantize_result(0, y_woven[0])
-        y_woven[3] = weave_result(3)
-        quantize_result(1, y_woven[1])
-        quantize_result(2, y_woven[2])
+        second_layer(0, 0, nc.scalar.copy)
+        store_result(0, slice(0, 1))
+        second_layer(0, 1, nc.scalar.copy)
+        store_result(0, slice(1, 2))
+        second_layer(0, 2, nc.vector.tensor_copy)
+        second_layer(0, 3, nc.vector.tensor_copy)
+        store_result(0, slice(2, PACK))
+        y_woven = {}
+        for t in range(PACK):
+            second_layer(1, t, nc.vector.tensor_copy if t % 2 else nc.scalar.copy)
+        store_result(1, slice(0, PACK))
+        y_woven[0] = weave_result(0, nc.scalar.copy)
+        y_woven[1] = weave_result(1, nc.vector.tensor_copy)
+        y_woven[2] = weave_result(2, nc.scalar.copy)
+        y_woven[3] = weave_result(3, nc.vector.tensor_copy)
+        for c in range(LAST):
+            quantize_result(c, y_woven[c])
         nc.sync.dma_start(out_words[:, : LAST * CHUNK], y_words[:, : LAST * CHUNK].bitcast(I32))
-        quantize_result(3, y_woven[3])
+        quantize_result(LAST, y_woven[LAST])
         nc.sync.dma_start(out_words[:, LAST * CHUNK :], y_words[:, LAST * CHUNK :].bitcast(I32))
         for q in range(4):
             queue = nc.sync if q % 2 == 0 else nc.scalar

@@ -95,10 +95,10 @@ def tile_picked_zedge_silu_po_kernel(tc, x_words, x_scales, eT, w1, w2, w3, w4, 
         w3_q = [quantize_pair(w3_dealt[u], f"w3_{u}") for u in range(2)]
         w2_q.append(quantize_pair(w2_dealt[1], "w2_1", tag="w3_raw0"))
 
-        def weave(dst_tile, src, copy=nc.vector.tensor_copy):
+        def weave(dst_tile, src, copy, run):
             copy(
-                dst_tile.rearrange("p (c i t) -> p c t i", i=2, t=PACK),
-                src.rearrange("p t (c i) -> p c t i", i=2),
+                dst_tile.rearrange("p (c i t) -> p c t i", i=run, t=PACK),
+                src.rearrange("p t (c i) -> p c t i", i=run),
             )
 
         e_words = sb([P, S], U32, "e_words")
@@ -106,11 +106,12 @@ def tile_picked_zedge_silu_po_kernel(tc, x_words, x_scales, eT, w1, w2, w3, w4, 
         h_scales = sb([P, S], U8, "h_scales")
         e_woven = [sb([P, PACK * CHUNK], BF16, f"e_woven{c}") for c in range(CHUNKS)]
 
-        def weave_edges(c, first, count, copy):
+        def weave_edges(c, first, count, copy, run):
             weave(
                 e_woven[c][:, PACK * first : PACK * (first + count)],
                 e_raw[:, :, c * CHUNK + first : c * CHUNK + first + count],
                 copy,
+                run,
             )
 
         def quantize_edges(c):
@@ -118,12 +119,12 @@ def tile_picked_zedge_silu_po_kernel(tc, x_words, x_scales, eT, w1, w2, w3, w4, 
             nc.vector.quantize_mx(out=e_words[:, cols].bitcast(FP8X4), scales=e_scales[:, cols], in_=e_woven[c][:])
 
         half_chunk = CHUNK // 2
-        weave_edges(0, 0, half_chunk, nc.vector.tensor_copy)
-        weave_edges(0, half_chunk, half_chunk, nc.scalar.copy)
-        weave_edges(1, 0, CHUNK, nc.vector.tensor_copy)
-        weave_edges(2, 0, CHUNK, nc.scalar.copy)
+        weave_edges(0, 0, half_chunk, nc.vector.tensor_copy, 2)
+        weave_edges(0, half_chunk, half_chunk, nc.scalar.copy, 4)
+        weave_edges(1, 0, CHUNK, nc.vector.tensor_copy, 2)
+        weave_edges(2, 0, CHUNK, nc.scalar.copy, 4)
         quantize_edges(0)
-        weave_edges(3, 0, CHUNK, nc.scalar.copy)
+        weave_edges(3, 0, CHUNK, nc.scalar.copy, 4)
         for c in range(1, CHUNKS):
             quantize_edges(c)
 
@@ -198,9 +199,9 @@ def tile_picked_zedge_silu_po_kernel(tc, x_words, x_scales, eT, w1, w2, w3, w4, 
         def result_chunk(c):
             return ys[c // 2][:, :, c % 2 * CHUNK : (c % 2 + 1) * CHUNK]
 
-        def weave_result(c, copy):
+        def weave_result(c, copy, run):
             woven = sb([P, PACK * CHUNK], BF16, f"y_woven{c}")
-            weave(woven[:], result_chunk(c), copy)
+            weave(woven[:], result_chunk(c), copy, run)
             return woven
 
         def store_result(b, slices):
@@ -243,10 +244,10 @@ def tile_picked_zedge_silu_po_kernel(tc, x_words, x_scales, eT, w1, w2, w3, w4, 
         for t in range(PACK):
             second_layer(1, t, nc.vector.tensor_copy if t % 2 else nc.scalar.copy)
         store_result(1, slice(0, PACK))
-        y_woven[0] = weave_result(0, nc.scalar.copy)
-        y_woven[1] = weave_result(1, nc.vector.tensor_copy)
-        y_woven[2] = weave_result(2, nc.scalar.copy)
-        y_woven[3] = weave_result(3, nc.vector.tensor_copy)
+        y_woven[0] = weave_result(0, nc.scalar.copy, 4)
+        y_woven[1] = weave_result(1, nc.vector.tensor_copy, 2)
+        y_woven[2] = weave_result(2, nc.scalar.copy, 4)
+        y_woven[3] = weave_result(3, nc.vector.tensor_copy, 2)
         for c in range(LAST):
             quantize_result(c, y_woven[c])
         nc.sync.dma_start(out_words[:, : LAST * CHUNK], y_words[:, : LAST * CHUNK].bitcast(I32))

@@ -34,11 +34,11 @@ def tile_picked_zedge_silu_po_kernel(tc, x_words, x_scales, eT, w1, w2, w3, w4, 
             return keep.tile(shape, dtype, name=name, tag=tag or name, align_bytes=64)
 
         node_scales = sb([P, T], U8, "node_scales")
-        nc.gpsimd.memset(node_scales[:].bitcast(I32), 0)
+        nc.vector.memset(node_scales[:].bitcast(I32), 0)
 
         warm_in = sb([P, 1], F32, "warm_in")
         warm_out = sb([P, 1], F32, "warm_out")
-        nc.gpsimd.memset(warm_in[:], 0.0)
+        nc.vector.memset(warm_in[:], 0.0)
         nc.scalar.activation(warm_out[:], warm_in[:], SILU)
 
         node_words = sb([P, T], U32, "node_words")

@@ -31,7 +31,7 @@ def tile_picked_zedge_silu_po_kernel(tc, x_words, x_scales, eT, w1, w2, w3, w4, 
         psum = ctx.enter_context(tc.psum_pool(name="psum", bufs=1))
 
         def sb(shape, dtype, name, tag=None):
-            return keep.tile(shape, dtype, name=name, tag=tag or name, align_bytes=64)
+            return keep.tile(shape, dtype, name=name, tag=tag or name, align_bytes=256)
 
         node_scales = sb([P, T], U8, "node_scales")
         nc.vector.memset(node_scales[:].bitcast(I32), 0)

@@ -31,7 +31,7 @@ def tile_picked_zedge_silu_po_kernel(tc, x_words, x_scales, eT, w1, w2, w3, w4, 
         psum = ctx.enter_context(tc.psum_pool(name="psum", bufs=1))
 
         def sb(shape, dtype, name, tag=None):
-            return keep.tile(shape, dtype, name=name, tag=tag or name, align_bytes=256)
+            return keep.tile(shape, dtype, name=name, tag=tag or name, align_bytes=1024)
 
         node_scales = sb([P, T], U8, "node_scales")
         nc.vector.memset(node_scales[:].bitcast(I32), 0)

from contextlib import ExitStack

import concourse.mybir as mybir

K, T, S, H, N = 512, 1024, 512, 512, 512
FLOPS = 2 * K * H * S * 3 + 2 * H * N * S

F32 = mybir.dt.float32
BF16 = mybir.dt.bfloat16
I32 = mybir.dt.int32
U32 = mybir.dt.uint32
U16 = mybir.dt.uint16
U8 = mybir.dt.uint8
FP8X4 = mybir.dt.float8_e4m3fn_x4
SILU = mybir.ActivationFunctionType.Silu

P = 128
PACK = 4
CHUNK = 128
CHUNKS = S // CHUNK
LAST = CHUNKS - 1
HALF = S // 2
SENDER, RECEIVER, EDGE = 0, 1, 2


def tile_picked_zedge_silu_po_kernel(tc, x_words, x_scales, eT, w1, w2, w3, w4, offs, dst, out_0, out_1, out_2):
    nc = tc.nc
    with ExitStack() as ctx:
        lists = ctx.enter_context(tc.tile_pool(name="lists", bufs=1))
        keep = ctx.enter_context(tc.tile_pool(name="keep", bufs=1))
        psum = ctx.enter_context(tc.psum_pool(name="psum", bufs=1))

        def sb(shape, dtype, name, tag=None):
            return keep.tile(shape, dtype, name=name, tag=tag or name, align_bytes=1024)

        node_scales = sb([P, T], U8, "node_scales")
        nc.vector.memset(node_scales[:].bitcast(I32), 0)

        warm_in = sb([P, 1], F32, "warm_in")
        warm_out = sb([P, 1], F32, "warm_out")
        nc.vector.memset(warm_in[:], 0.0)
        nc.scalar.activation(warm_out[:], warm_in[:], SILU)

        node_words = sb([P, T], U32, "node_words")
        nc.sync.dma_start(node_words[:].bitcast(I32), x_words[0].rearrange("p n t -> p (n t)").bitcast(I32))
        senders = lists.tile([P, S // 16], U16, name="senders")
        receivers = lists.tile([P, S // 16], U16, name="receivers")
        nc.sync.dma_start(senders[:], offs)
        nc.sync.dma_start(receivers[:], dst)
        for q in range(4):
            nc.scalar.dma_start(node_scales[32 * q : 32 * q + 4, :].bitcast(I32), x_scales[0, 4 * q : 4 * q + 4, :].bitcast(I32))

        def load(w, name, first, width):
            raw = sb([P, PACK, width], F32, f"{name}_raw{first}")
            nc.sync.dma_start(raw[:], w.rearrange("(p j) c -> p j c", j=PACK)[:, :, first : first + width])
            return raw

        w1_raw = load(w1, "w1", 0, H)
        w2_raw = load(w2, "w2", 0, H)
        w3_raw = load(w3, "w3", 0, H)
        e_raw = load(eT, "e", 0, S)
        w4_raw = [load(w4, "w4", 0, N // 2), load(w4, "w4", N // 2, N // 2)]

        picked = []
        for name, offsets in (("sender", senders), ("receiver", receivers)):
            words = sb([P, S], U32, name + "_words")
            nc.vector.tensor_copy(words[:], node_words[:].indirect(offsets[:]))
            picked.append([words])
        for i, (name, offsets) in enumerate((("sender", senders), ("receiver", receivers))):
            scales = sb([P, S], U8, name + "_scales")
            nc.vector.tensor_copy(scales[:], node_scales[:].indirect(offsets[:]))
            picked[i].append(scales)

        def pair(raw, u):
            return raw[:].rearrange("p j (m u v) -> p u m j v", u=2, v=2)[:, u]

        def deal(copy, src, name, tag=None):
            dealt = sb([P, 2, src.shape[1], PACK], BF16, name, tag=tag)
            copy(dealt[:].rearrange("p v m j -> p m j v"), src)
            return dealt

        def quantize_pair(dealt, name, tag=None):
            words = sb([P, 2 * P], U32, name + "_words", tag=tag)
            scales = sb([P, 2 * P], U8, name + "_scales")
            nc.vector.quantize_mx(
                out=words[:].bitcast(FP8X4), scales=scales[:], in_=dealt[:].rearrange("p v m j -> p (v m j)")
            )
            return words, scales

        w1_dealt = [deal(nc.scalar.copy, pair(w1_raw, u), f"w1_dealt{u}") for u in range(2)]
        w1_q = [quantize_pair(w1_dealt[u], f"w1_{u}") for u in range(2)]
        w2_dealt = [deal(nc.scalar.copy, pair(w2_raw, 0), "w2_dealt0"), deal(nc.vector.tensor_copy, pair(w2_raw, 1), "w2_dealt1")]
        w2_q = [quantize_pair(w2_dealt[0], "w2_0")]
        w3_dealt = [deal(nc.vector.tensor_copy, pair(w3_raw, 0), "w3_dealt0"), deal(nc.scalar.copy, pair(w3_raw, 1), "w3_dealt1")]
        w3_q = [quantize_pair(w3_dealt[u], f"w3_{u}") for u in range(2)]
        w2_q.append(quantize_pair(w2_dealt[1], "w2_1", tag="w3_raw0"))

        def weave(dst_tile, src, copy, run):
            copy(
                dst_tile.rearrange("p (c i t) -> p c t i", i=run, t=PACK),
                src.rearrange("p t (c i) -> p c t i", i=run),
            )

        e_words = sb([P, S], U32, "e_words")
        e_scales = sb([P, S], U8, "e_scales")
        h_scales = sb([P, S], U8, "h_scales")
        e_woven = [sb([P, PACK * CHUNK], BF16, f"e_woven{c}") for c in range(CHUNKS)]

        def weave_edges(c, first, count, copy, run):
            weave(
                e_woven[c][:, PACK * first : PACK * (first + count)],
                e_raw[:, :, c * CHUNK + first : c * CHUNK + first + count],
                copy,
                run,
            )

        def quantize_edges(c):
            cols = slice(c * CHUNK, (c + 1) * CHUNK)
            nc.vector.quantize_mx(out=e_words[:, cols].bitcast(FP8X4), scales=e_scales[:, cols], in_=e_woven[c][:])

        half_chunk = CHUNK // 2
        weave_edges(0, 0, half_chunk, nc.vector.tensor_copy, 2)
        weave_edges(0, half_chunk, half_chunk, nc.scalar.copy, 4)
        weave_edges(1, 0, CHUNK, nc.vector.tensor_copy, 2)
        weave_edges(2, 0, CHUNK, nc.scalar.copy, 4)
        quantize_edges(0)
        weave_edges(3, 0, CHUNK, nc.scalar.copy, 4)
        for c in range(1, CHUNKS):
            quantize_edges(c)

        w4_words = sb([P, N], U32, "w4_words")
        w4_scales = sb([P, N], U8, "w4_scales")

        def quantize_w4(half, u, dealt):
            for v in range(2):
                first = (2 * u + v) * P + half * (P // 2)
                cols = slice(first, first + P // 2)
                nc.vector.quantize_mx(
                    out=w4_words[:, cols].bitcast(FP8X4),
                    scales=w4_scales[:, cols],
                    in_=dealt[:, v].rearrange("p m j -> p (m j)"),
                )

        moving = [picked[0], picked[1], [e_words, e_scales]]
        stationary = [w1_q, w2_q, w3_q]
        pre = [psum.tile([P, PACK, CHUNK], F32, name=f"pre{c}") for c in range(CHUNKS)]

        def first_pass(c, t, g):
            cols = slice(c * CHUNK, (c + 1) * CHUNK)
            rows = slice(t % 2 * P, (t % 2 + 1) * P)
            nc.tensor.matmul_mx(
                out=pre[c][:, t, :],
                lhsT=stationary[g][t // 2][0][:, rows].bitcast(FP8X4),
                lhsT_scale=stationary[g][t // 2][1][:, rows],
                rhs=moving[g][0][:, cols].bitcast(FP8X4),
                rhs_scale=moving[g][1][:, cols],
                start=(g == SENDER and t == 0),
                stop=(g == (RECEIVER if c == LAST else EDGE) and t == PACK - 1),
            )

        hiddens = []

        def first_layer(c):
            for g in (EDGE, RECEIVER) if c == LAST else (EDGE,):
                for t in range(PACK):
                    first_pass(c, t, g)
            hidden = sb([P, PACK * CHUNK], BF16, f"hidden{c}")
            hiddens.append(hidden)
            nc.scalar.activation(
                hidden[:].rearrange("p (n t) -> p n t", t=PACK), pre[c][:].rearrange("p t n -> p n t"), SILU
            )

        y_words = sb([P, S], U32, "y_words")
        y_scales = sb([P, S], U8, "y_scales")
        out_rows = out_0.rearrange("(p t) n -> p t n", t=PACK)
        out_words = out_1[0].rearrange("p n t -> p (n t)").bitcast(I32)

        def quantize_hidden(c):
            cols = slice(c * CHUNK, (c + 1) * CHUNK)
            words = h_words[c // 2][:, c % 2 * CHUNK : (c % 2 + 1) * CHUNK]
            nc.vector.quantize_mx(out=words.bitcast(FP8X4), scales=h_scales[:, cols], in_=hiddens[c][:])

        ys = [sb([P, PACK, HALF], F32, f"y{b}") for b in range(2)]

        def second_layer(b, t, copy):
            acc = psum.tile([P, HALF], F32, name=f"acc{b}{t}", tag=f"pre{t}" if b else f"acc{t}")
            rows = slice(t * P, (t + 1) * P)
            nc.tensor.matmul_mx(
                out=acc[:],
                lhsT=w4_words[:, rows].bitcast(FP8X4),
                lhsT_scale=w4_scales[:, rows],
                rhs=h_words[b][:].bitcast(FP8X4),
                rhs_scale=h_scales[:, b * HALF : (b + 1) * HALF],
                start=True,
                stop=True,
            )
            copy(ys[b][:, t], acc[:])

        def result_chunk(c):
            return ys[c // 2][:, :, c % 2 * CHUNK : (c % 2 + 1) * CHUNK]

        def weave_result(c, copy, run):
            woven = sb([P, PACK * CHUNK], BF16, f"y_woven{c}")
            weave(woven[:], result_chunk(c), copy, run)
            return woven

        def store_result(b, slices):
            nc.sync.dma_start(out_rows[:, slices, b * HALF : (b + 1) * HALF], ys[b][:, slices])

        def quantize_result(c, woven):
            cols = slice(c * CHUNK, (c + 1) * CHUNK)
            nc.vector.quantize_mx(out=y_words[:, cols].bitcast(FP8X4), scales=y_scales[:, cols], in_=woven[:])

        for g, chunks in ((SENDER, CHUNKS), (RECEIVER, LAST)):
            for t in range(PACK):
                for c in range(chunks):
                    first_pass(c, t, g)
        for c in range(CHUNKS):
            first_layer(c)

        w4_first = [deal(nc.vector.tensor_copy, pair(w4_raw[0], u), f"w4_dealt0{u}") for u in range(2)]
        for u in range(2):
            quantize_w4(0, u, w4_first[u])
        h_words = [sb([P, HALF], U32, "h_first", tag="w4_dealt00")]
        quantize_hidden(0)
        w4_second = [
            deal(nc.vector.tensor_copy, pair(w4_raw[1], u), f"w4_dealt1{u}", tag=("w4_dealt01", "hidden0")[u]) for u in range(2)
        ]
        quantize_hidden(1)
        for u in range(2):
            quantize_w4(1, u, w4_second[u])
        h_words.append(sb([P, HALF], U32, "h_rest", tag="w4_raw256"))
        quantize_hidden(2)
        quantize_hidden(3)

        second_layer(0, 0, nc.scalar.copy)
        store_result(0, slice(0, 1))
        second_layer(0, 1, nc.scalar.copy)
        store_result(0, slice(1, 2))
        second_layer(0, 2, nc.vector.tensor_copy)
        second_layer(0, 3, nc.vector.tensor_copy)
        store_result(0, slice(2, PACK))
        y_woven = {}
        for t in range(PACK):
            second_layer(1, t, nc.vector.tensor_copy if t % 2 else nc.scalar.copy)
        store_result(1, slice(0, PACK))
        y_woven[0] = weave_result(0, nc.scalar.copy, 4)
        y_woven[1] = weave_result(1, nc.vector.tensor_copy, 2)
        y_woven[2] = weave_result(2, nc.scalar.copy, 4)
        y_woven[3] = weave_result(3, nc.vector.tensor_copy, 2)
        for c in range(LAST):
            quantize_result(c, y_woven[c])
        nc.sync.dma_start(out_words[:, : LAST * CHUNK], y_words[:, : LAST * CHUNK].bitcast(I32))
        quantize_result(LAST, y_woven[LAST])
        nc.sync.dma_start(out_words[:, LAST * CHUNK :], y_words[:, LAST * CHUNK :].bitcast(I32))
        for q in range(4):
            queue = nc.sync if q % 2 == 0 else nc.scalar
            queue.dma_start(out_2[0, 4 * q : 4 * q + 4, :].bitcast(I32), y_scales[32 * q : 32 * q + 4, :].bitcast(I32))
